import numpy as np, ml_dtypes
CORES = [10,34,74,98]
N = 4
import mx_ref
BF = ml_dtypes.bfloat16
def entries(a):
    return np.ascontiguousarray(a.T).reshape(-1)
def table(e):
    return np.ascontiguousarray(np.reshape(e, (-1, 16)).T).astype(np.int32)
def gcols(t, e):
    v = np.concatenate([t.reshape(8, 16, -1, 4), np.zeros((8, 16, 1, 4), BF)], axis=2)
    return np.ascontiguousarray(np.stack([v[g][:, e[g]] for g in range(8)])).reshape(128, -1)
def cut(t, i, w=512):
    return t[:, w * i:w * i + w]
def f(rng, *shape):
    return mx_ref.flush((rng.standard_normal(shape, dtype=np.float32) * np.exp2(rng.integers(-2, 3, shape[:-1] + (1,)))).astype(BF))
def wide(rng, *shape, cols=0):
    v = rng.standard_normal(shape, dtype=np.float32) * np.exp2(rng.integers(-12, 13, shape)).astype(np.float32)
    if cols: v *= np.repeat(np.exp2(rng.integers(-cols, cols + 1, shape[:-2] + (1, shape[-1] // 4))) * (rng.random(shape[:-2] + (1, shape[-1] // 4)) > 0.0625), 4, axis=-1).astype(np.float32)
    return mx_ref.flush(v.astype(BF))
K, T, O = 512, 512, 3
SH = (7, 6, 5, 4, 3, 2, 1, 0)
A = (1531, 797, 1877, 1129, 619, 1993, 1367, 911)
B = (1013, 1741, 587, 1459, 1907, 733, 1229, 1667)
def levels(q):
    return list(range(8 // N * q, 8 // N * (q + 1)))
def owned(t):
    t = t.reshape(N, 8, 16, -1).copy()
    for q in range(N):
        for g in range(8):
            if g not in levels(q): t[q, g] = 0
    return t.reshape(N, 128, -1)
def pack(p):
    return np.stack([table(p[r]) for r in range(N)])
def places(rng):
    return {"px": pack(rng.integers(0, 1024, (N, T))), "py": pack(rng.integers(0, 1024, (N, T)))}
def setup_inputs(rng):
    return {"tb": owned(f(rng, N, 128, 4 * K)), **places(rng), "w": f(rng, N, 128, 512 * O)}
def setup_inputs_same(rng):
    d = setup_inputs(rng)
    d["px"] = pack(np.repeat(rng.integers(0, 1024, (N, 1)), T, axis=1)); d["py"] = pack(np.repeat(rng.integers(0, 1024, (N, 1)), T, axis=1))
    return d
def setup_inputs_corner(rng):
    d = setup_inputs(rng); c = rng.integers(0, 4, (N, T))
    for r in range(N): c[r, rng.permutation(T)[:4]] = np.arange(4)
    d["px"] = pack((c & 1) * 1023); d["py"] = pack((c >> 1) * 1023)
    return d
def setup_inputs_alike(rng):
    d = setup_inputs(rng)
    d["px"] = pack(np.repeat(rng.integers(0, 1024, (1, T)), N, axis=0)); d["py"] = pack(np.repeat(rng.integers(0, 1024, (1, T)), N, axis=0))
    return d
def setup_inputs_line(rng):
    d = setup_inputs(rng)
    d["px"] = pack(rng.integers(0, 1025 - T, (N, 1)) + np.arange(T)); d["py"] = pack(np.repeat(rng.integers(0, 1024, (N, 1)), T, axis=1))
    return d
def setup_inputs_spread(rng):
    d = setup_inputs(rng); d["tb"] = owned(wide(rng, N, 128, 4 * K, cols=4)); return d
def check_inputs(d):
    b = []
    for r in range(N):
        for n in ("px", "py"):
            e = entries(d[n][r])
            if e.min() < 0 or e.max() > 1023: b.append(n)
        t = d["tb"][r].reshape(8, 16, -1).astype(np.float32)
        if any((t[g] != 0).any() for g in range(8) if g not in levels(r)): b.append("tb")
    return b
def addresses(x, y):
    return np.stack([((x >> SH[g]) * A[g] + (y >> SH[g]) * B[g]) & (K - 1) for g in range(8)])
def reference(tb, px, py, w):
    y = np.zeros((N, 128, O * T), np.float32)
    for r in range(N):
        e = addresses(entries(px[r]), entries(py[r])); E = []
        for q in range(N):
            a = np.full((8, T), -1); a[levels(q)] = e[levels(q)]
            E.append(mx_ref.quantize(np.ascontiguousarray(gcols(tb[q], a))))
        for o in range(O):
            W = mx_ref.quantize(np.ascontiguousarray(cut(w[r], o)))
            Z = mx_ref.matmul(W, E[0])
            for q in range(1, N): Z = Z + mx_ref.matmul(W, E[q])
            y[r][:, T * o:T * o + T] = Z
    return {"y": y}

@@ -1,0 +1,294 @@
+from concourse.bass import DstId, RemoteDMATransfer
+from concourse.mybir import dt, AluOpType, ActivationFunctionType
+
+N = 4
+O = 3
+SH = (7, 6, 5, 4, 3, 2, 1, 0)
+MA = (1531, 797, 1877, 1129, 619, 1993, 1367, 911)
+MB = (1013, 1741, 587, 1459, 1907, 733, 1229, 1667)
+K = 512
+M0 = (0, 11, 21)
+C = 11
+NC = 16 * C
+F8 = "float8_e4m3fn_x4"
+
+SCRATCH = {
+    "cxy": ("sbuf", [128, 64], "int32"),
+    "pw": ("sbuf", [128, 16], "int32"), "lw": ("sbuf", [128, 16], "int32"), "ab": ("sbuf", [128, 8 * C], "float32"),
+    "sc": ("sbuf", [128, 4], "float32"), "bc": ("sbuf", [128, 4], "float32"),
+    "xs": ("sbuf", [128, 8 * C], "int32"), "xm": ("sbuf", [128, 8 * C], "float32"),
+    "xa": ("sbuf", [128, 4 * C], "int32"), "adr": ("sbuf", [128, 4 * C], "int32"),
+    "lout": ("sbuf", [128, 48], "uint16"), "lin": ("sbuf", [128, 48], "uint16"),
+    "tbl": ("sbuf", [128, 4 * K], "bfloat16"), "zb": ("sbuf", [128, 512], "bfloat16"),
+    "yb": ("sbuf", [128, 1536], "float32"), "part": ("sbuf", [128, 2 * NC], "float32"),
+    "acc": ("psum", [128, 4096], "float32"),
+}
+for _t in (1, 2, 3):
+    SCRATCH["off%d" % _t] = ("sbuf", [128, 48], "uint16")
+for _i in range(6):
+    SCRATCH["wt%d" % _i] = ("sbuf", [128, 1536], "bfloat16")
+    SCRATCH["wq%d" % _i] = ("sbuf", [128, 384], F8)
+    SCRATCH["ws%d" % _i] = ("sbuf", [128, 384], "uint8")
+for _k in range(4):
+    SCRATCH["eb%d" % _k] = ("sbuf", [128, 4 * NC], "bfloat16")
+    SCRATCH["eq%d" % _k] = ("sbuf", [128, NC], F8)
+    SCRATCH["es%d" % _k] = ("sbuf", [128, NC], "uint8")
+    if _k:
+        SCRATCH["rq%d" % _k] = ("sbuf", [128, NC], F8)
+        SCRATCH["rs%d" % _k] = ("sbuf", [128, NC], "uint8")
+
+SEMAPHORES = (["lx", "ly", "fz", "tbs", "iot", "ct", "cd", "ad", "lo", "lown", "larr", "lsent", "esent",
+               "pr", "rv", "pb", "vb", "sf", "vf", "ys"]
+              + ["%s%d" % (n, k) for n in ("gv", "gs", "qe", "oo", "oi", "arr") for k in range(4)]
+              + ["%s%d" % (n, i) for n in ("fw", "dw", "qw") for i in range(6)]
+              + ["pp%d" % b for b in range(9)])
+
+ADD, MUL, AND = AluOpType.add, AluOpType.mult, AluOpType.bitwise_and
+COPY = ActivationFunctionType.Copy
+
+
+def rank_program(g, core, T, topo):
+    r = T.rank_of(core)
+    if r is None:
+        return
+    S = T.sem
+    V, A, P, Y = g.vector, g.scalar, g.tensor, g.sync
+    ks = sorted((1, 2, 3), key=lambda k: topo.same_plane(topo.chip(core), topo.chip(T.cores[r ^ k])))
+    k1, k2, k3 = ks
+    q1, q2, q3 = [r ^ k for k in ks]
+    tiles = [{r, q1}, {r, q2}, {r, q3}, {q1, q2}, {q1, q3}, {q2, q3}]
+    dsts = [T.cores[q] for q in (q1, q2, q3)]
+    engs = [e for e in topo.engines(core, dsts[0]) if all(e in topo.engines(core, d) for d in dsts)]
+    ne = len(engs)
+    mask = sum(1 << e for e in engs)
+    parts = [engs[0::2], engs[1::4], engs[3::4]]
+
+    for s in range(4):
+        for l in range(2):
+            p = 32 * s + 16 * l
+            if s < 3:
+                m = M0[s]
+                Y.dma_start(T.cxy[p:p + 16, 0:C], T.px[:, m:m + C]).then_inc(S.lx, 16)
+                A.dma_start(T.cxy[p:p + 16, C:2 * C], T.py[:, m:m + C]).then_inc(S.ly, 16)
+            else:
+                Y.dma_start(T.cxy[p:p + 16, 0:32], T.px[:]).then_inc(S.lx, 16)
+                A.dma_start(T.cxy[p:p + 16, 32:64], T.py[:]).then_inc(S.ly, 16)
+    for s in range(4):
+        q = r if s != r else (r + 1) % N
+        Y.dma_start(T.tbl[32 * s:32 * s + 32, :], T.tb[32 * q:32 * q + 32, :]).then_inc(S.tbs, 16)
+
+    def wload(i, n):
+        Y.wait_ge(S["fw%d" % i], n)
+        a, b = sorted(tiles[i])
+        for q, s in ((a, b), (b, a)):
+            Y.dma_start(T["wt%d" % i][32 * s:32 * s + 32, :], T.w[32 * q:32 * q + 32, :]).then_inc(S["dw%d" % i], 16)
+
+    wload(0, 1)
+    wload(2, 3)
+    wload(1, 2)
+    Y.wait_ge(S.lsent, ne)
+    for i, n in ((3, 3), (4, 3), (5, 1)):
+        wload(i, n)
+
+    g.iota(T.pw[:], [[0, 16]], 0, 1).then_inc(S.iot, 1)
+    trs = []
+    for k, q, d, es in zip(ks, (q1, q2, q3), dsts, parts):
+        rid, pid, _ = topo.addr(d)
+        trs.append(RemoteDMATransfer(
+            dst_ids=[DstId(rid=rid, pnc=pid)], dma_engine_mask=sum(1 << e for e in es), remote_sem=S.larr,
+            srcs=[T.lout[:, 12 * q:12 * q + 12]], dsts=[T.lin[:, 12 * k:12 * k + 12]]))
+    g.wait_ge(S.lo, 3)
+    g.remote_dma_fused(trs, local_sem=S.lsent)
+    for k, d in zip(ks, dsts):
+        rid, pid, _ = topo.addr(d)
+        g.wait_ge(S["qe%d" % k], 1)
+        g.remote_dma(T["rq%d" % k][:].bitcast(dt.uint8), T["eq%d" % k][:].bitcast(dt.uint8), S["arr%d" % k], S.esent, pid, rid, mask)
+        g.remote_dma(T["rs%d" % k][:], T["es%d" % k][:], S["arr%d" % k], S.esent, pid, rid, mask)
+    g.wait_ge(S.esent, 6 * ne)
+
+    V.memset(T.zb[:], 0.0).then_inc(S.fz, 1)
+    V.memset(T.wt0[:], 0.0).then_inc(S.fw0, 1)
+    V.memset(T.lout[:], 0).then_inc(S.cd, 1)
+    V.memset(T.xs[96:128, :], 0).then_inc(S.cd, 1)
+    V.wait_ge(S.iot, 1)
+    V.tensor_scalar(T.lw[:], T.pw[:], 16, None, AND).then_inc(S.ct, 1)
+    V.wait_ge(S.ct, 1)
+    for q in range(N):
+        a, b = 2 * q, 2 * q + 1
+        V.tensor_scalar(T.sc[:, q:q + 1], T.lw[:, 0:1], 2.0 ** -SH[a] / 16.0, 2.0 ** -SH[a], MUL, ADD).then_inc(S.cd, 1)
+        for c, M in ((0, MA), (4 * C, MB)):
+            V.tensor_scalar(T.ab[:, c + q:c + 4 * C:4], T.lw[:, 0:C], (M[b] - M[a]) / 4.0, 4.0 * M[a], MUL, ADD).then_inc(S.cd, 1)
+    V.wait_ge(S.cd, 14)
+    V.tensor_scalar(T.bc[:], T.sc[:], 0.5, -0.5, MUL, ADD).then_inc(S.cd, 1)
+    V.memset(T.wt1[:, 0:512], 0.0).then_inc(S.fw1, 1)
+    V.wait_ge(S.cd, 15)
+    V.wait_ge(S.lx, 128)
+    V.wait_ge(S.ly, 128)
+    for q in range(N):
+        V.tensor_scalar(T.xs[0:96, q:8 * C:4], T.cxy[0:96, 0:2 * C], T.sc[0:96, q:q + 1], T.bc[0:96, q:q + 1], MUL, ADD).then_inc(S.ad, 1)
+        if q < 3:
+            m = M0[q]
+            for c, x in ((0, m), (4 * C, 32 + m)):
+                V.tensor_scalar(T.xs[96:128, c + q:c + 4 * C:4], T.cxy[96:128, x:x + C], T.sc[96:128, q:q + 1], T.bc[96:128, q:q + 1], MUL, ADD).then_inc(S.ad, 1)
+    V.wait_ge(S.ad, 10)
+    V.tensor_tensor(T.xm[:], T.xs[:], T.ab[:], MUL).then_inc(S.ad, 1)
+    V.wait_ge(S.ad, 11)
+    V.tensor_tensor(T.xa[:], T.xm[:, 0:4 * C], T.xm[:, 4 * C:8 * C], ADD).then_inc(S.ad, 1)
+    V.wait_ge(S.ad, 12)
+    V.tensor_scalar(T.adr[:], T.xa[:], 4 * (K - 1), None, AND).then_inc(S.ad, 1)
+    V.wait_ge(S.ad, 13)
+    for q in (q1, q2, q3, r):
+        V.tensor_copy(T.lout[:, 12 * q:12 * q + C], T.adr[:, q:4 * C:4]).then_inc(S.lown if q == r else S.lo, 1)
+    V.memset(T.wt1[:, 512:1536], 0.0).then_inc(S.fw1, 1)
+
+    def offs(t, k):
+        c = 12 * k
+        if t:
+            return T["off%d" % t][:, c:c + C]
+        return T.lin[:, c:c + C] if k else T.lout[:, 12 * r:12 * r + C]
+
+    V.wait_ge(S.lown, 1)
+    for t in (3, 1, 2):
+        V.tensor_scalar(T["off%d" % t][:, 0:12], T.lout[:, 12 * r:12 * r + 12], float(t), None, ADD).then_inc(S["oo%d" % t], 1)
+
+    def vg(k):
+        for t in (1, 2):
+            V.tensor_copy(T["eb%d" % k][:, t:4 * NC:4], T.tbl[:].indirect(offs(t, k))).then_inc(S["gv%d" % k], 1)
+
+    def vq(k):
+        if k:
+            V.wait_ge(S["gv%d" % k], 2)
+        V.wait_ge(S["gs%d" % k], 2 if k else 4)
+        V.quantize_mx(T["eq%d" % k][:], T["es%d" % k][:], T["eb%d" % k][:]).then_inc(S["qe%d" % k], 1)
+
+    def vw(i):
+        V.wait_ge(S["dw%d" % i], 32)
+        V.quantize_mx(T["wq%d" % i][:], T["ws%d" % i][:], T["wt%d" % i][:]).then_inc(S["qw%d" % i], 1)
+
+    vw(0)
+    vw(2)
+    V.memset(T.wt5[:], 0.0).then_inc(S.fw5, 1)
+    vq(0)
+    vw(1)
+    V.wait_ge(S.tbs, 64)
+    V.wait_ge(S.larr, ne)
+    for t in (3, 1, 2):
+        V.tensor_scalar(T["off%d" % t][:, 12:48], T.lin[:, 12:48], float(t), None, ADD).then_inc(S["oi%d" % t], 1)
+    V.wait_ge(S.oi1, 1)
+    V.wait_ge(S.oi2, 1)
+    for k in ks:
+        vg(k)
+        vq(k)
+    for i in (3, 4, 5):
+        vw(i)
+
+    A.wait_ge(S.fz, 1)
+    for i in (2, 3, 4):
+        for c in range(0, 1536, 512):
+            A.activation(T["wt%d" % i][:, c:c + 512], T.zb[:], COPY).then_inc(S["fw%d" % i], 1)
+    A.wait_ge(S.tbs, 64)
+
+    def ag(k, t):
+        A.activation(T["eb%d" % k][:, t:4 * NC:4], T.tbl[:].indirect(offs(t, k)), COPY).then_inc(S["gs%d" % k], 1)
+
+    A.wait_ge(S.lown, 1)
+    ag(0, 0)
+    for t in (3, 1, 2):
+        A.wait_ge(S["oo%d" % t], 1)
+        ag(0, t)
+    A.wait_ge(S.larr, ne)
+    for n, k in enumerate(ks):
+        ag(k, 0)
+        if n == 0:
+            A.wait_ge(S.oi3, 1)
+        ag(k, 3)
+
+    seq = [(0, 2), (0, 0), (0, 1), (1, 0), (1, 2), (1, 1), (2, 0), (2, 1), (2, 2)]
+    pas = [(0, 2), (1, 2)]
+    keep = [x for x in seq if x not in pas]
+
+    def base(x):
+        return 512 * (7 if x in pas else keep.index(x))
+
+    seen = []
+
+    def mm(k, x, first, last):
+        e, z = ("rq%d", "rs%d") if k else ("eq%d", "es%d")
+        o, th = x
+        q = r ^ k
+        s = 3 if (th == q and q < 3) else th
+        i = tiles.index({q, s})
+        if i not in seen:
+            seen.append(i)
+            P.wait_ge(S["qw%d" % i], 1)
+        c = slice(128 * o, 128 * o + 128)
+        b = base(x)
+        return P.matmul_mx(T.acc[:, b:b + NC], T["wq%d" % i][:, c], T["ws%d" % i][:, c], T[e % k][:], T[z % k][:], first, last)
+
+    P.wait_ge(S.qe0, 1)
+    for x in seq:
+        if x in pas:
+            if x == pas[1]:
+                P.wait_ge(S.rv, 1)
+            mm(0, x, True, True).then_inc(S.pr, 1)
+        else:
+            mm(0, x, True, False)
+    P.wait_ge(S["arr%d" % k1], 2 * ne)
+    for x in keep:
+        mm(k1, x, False, False)
+    P.wait_ge(S["arr%d" % k2], 2 * ne)
+    for x in seq:
+        if x in pas:
+            if x == pas[0]:
+                P.wait_ge(S.rv, 2)
+            else:
+                P.wait_ge(S.vb, 1)
+            mm(k1, x, True, False)
+            mm(k2, x, False, True).then_inc(S.pb, 1)
+        else:
+            mm(k2, x, False, False)
+    P.wait_ge(S["arr%d" % k3], 2 * ne)
+    for n, x in enumerate(seq):
+        if x in pas:
+            if x == pas[0]:
+                P.wait_ge(S.vb, 2)
+            else:
+                P.wait_ge(S.vf, 1)
+        mm(k3, x, x in pas, True).then_inc(S["pp%d" % n], 1)
+
+    for i in range(2):
+        A.wait_ge(S.pr, i + 1)
+        A.activation(T.part[:, NC * i:NC * i + NC], T.acc[:, 3584:3584 + NC], COPY).then_inc(S.rv, 1)
+    for i in range(2):
+        pi = T.part[:, NC * i:NC * i + NC]
+        V.wait_ge(S.pb, i + 1)
+        V.wait_ge(S.rv, i + 1)
+        V.tensor_tensor(pi, T.acc[:, 3584:3584 + NC], pi, ADD).then_inc(S.vb, 1)
+    cnt = {"s": 0, "v": 0}
+    done = {}
+    for n, x in enumerate(seq):
+        o, th = x
+        lo = 0 if th < 2 else 16 * (M0[1] + C - M0[2])
+        y = T.yb[:, 512 * o + 16 * M0[th] + lo:512 * o + 16 * M0[th] + NC]
+        b = base(x)
+        a = T.acc[:, b + lo:b + NC]
+        if x in pas:
+            i = pas.index(x)
+            V.wait_ge(S["pp%d" % n], 1)
+            V.wait_ge(S.vb, i + 1)
+            V.tensor_tensor(y, a, T.part[:, NC * i + lo:NC * i + NC], ADD).then_inc(S.vf, 1)
+            cnt["v"] += 1
+        elif n % 2:
+            A.wait_ge(S["pp%d" % n], 1)
+            A.activation(y, a, COPY).then_inc(S.sf, 1)
+            cnt["s"] += 1
+        else:
+            V.wait_ge(S["pp%d" % n], 1)
+            V.tensor_copy(y, a).then_inc(S.vf, 1)
+            cnt["v"] += 1
+        done[o] = (cnt["s"], cnt["v"])
+    for o in range(O):
+        Y.wait_ge(S.sf, done[o][0])
+        Y.wait_ge(S.vf, done[o][1])
+        Y.dma_start(T.y[:, 512 * o:512 * o + 512], T.yb[:, 512 * o:512 * o + 512]).then_inc(S.ys, 16)
+    Y.wait_ge(S.ys, 16 * O)

@@ -13,14 +13,15 @@ NC = 16 * C
 F8 = "float8_e4m3fn_x4"
 
 SCRATCH = {
-    "cxy": ("sbuf", [128, 64], "int32"),
-    "pw": ("sbuf", [128, 16], "int32"), "lw": ("sbuf", [128, 16], "int32"), "ab": ("sbuf", [128, 8 * C], "float32"),
-    "sc": ("sbuf", [128, 4], "float32"), "bc": ("sbuf", [128, 4], "float32"),
-    "xs": ("sbuf", [128, 8 * C], "int32"), "xm": ("sbuf", [128, 8 * C], "float32"),
-    "xa": ("sbuf", [128, 4 * C], "int32"), "adr": ("sbuf", [128, 4 * C], "int32"),
+    "cxy": ("sbuf", [128, 2, 32], "int32"),
+    "pw": ("sbuf", [128, 16], "int32"), "lw": ("sbuf", [128, 12], "int32"), "nz": ("sbuf", [128, 4], "int32"),
+    "lf": ("sbuf", [128, 12], "float32"), "uf": ("sbuf", [128, 4], "float32"),
+    "ab": ("sbuf", [128, 2, 48], "float32"), "sc": ("sbuf", [128, 4], "float32"), "bc": ("sbuf", [128, 4], "float32"),
+    "xs": ("sbuf", [128, 2, 48], "int32"), "xm": ("sbuf", [128, 2, 48], "float32"),
+    "xa": ("sbuf", [128, 48], "int32"), "adr": ("sbuf", [128, 48], "int32"),
     "lout": ("sbuf", [128, 48], "uint16"), "lin": ("sbuf", [128, 48], "uint16"),
     "tbl": ("sbuf", [128, 4 * K], "bfloat16"), "zb": ("sbuf", [128, 512], "bfloat16"),
-    "yb": ("sbuf", [128, 1536], "float32"), "part": ("sbuf", [128, 2 * NC], "float32"),
+    "yb": ("sbuf", [128, 1536], "float32"),
     "acc": ("psum", [128, 4096], "float32"),
 }
 for _t in (1, 2, 3):
@@ -29,22 +30,22 @@ for _i in range(6):
     SCRATCH["wt%d" % _i] = ("sbuf", [128, 1536], "bfloat16")
     SCRATCH["wq%d" % _i] = ("sbuf", [128, 384], F8)
     SCRATCH["ws%d" % _i] = ("sbuf", [128, 384], "uint8")
-for _k in range(4):
-    SCRATCH["eb%d" % _k] = ("sbuf", [128, 4 * NC], "bfloat16")
-    SCRATCH["eq%d" % _k] = ("sbuf", [128, NC], F8)
-    SCRATCH["es%d" % _k] = ("sbuf", [128, NC], "uint8")
-    if _k:
-        SCRATCH["rq%d" % _k] = ("sbuf", [128, NC], F8)
-        SCRATCH["rs%d" % _k] = ("sbuf", [128, NC], "uint8")
+for _j in range(4):
+    SCRATCH["eb%d" % _j] = ("sbuf", [128, 4 * NC], "bfloat16")
+    SCRATCH["eq%d" % _j] = ("sbuf", [128, NC], F8)
+    SCRATCH["es%d" % _j] = ("sbuf", [128, NC], "uint8")
+    if _j < 3:
+        SCRATCH["rq%d" % _j] = ("sbuf", [128, NC], F8)
+        SCRATCH["rs%d" % _j] = ("sbuf", [128, NC], "uint8")
 
-SEMAPHORES = (["lx", "ly", "fz", "tbs", "iot", "ct", "cd", "ad", "lo", "lown", "larr", "lsent", "esent",
-               "pr", "rv", "pb", "vb", "sf", "vf", "ys"]
-              + ["%s%d" % (n, k) for n in ("gv", "gs", "qe", "oo", "oi", "arr") for k in range(4)]
+SEMAPHORES = (["lx", "ly", "fz", "tz", "tbs", "iot", "c0", "c1", "c2", "ka", "kb", "ma", "mb", "sa", "sb", "loa", "lob",
+               "laa", "lab", "lsent", "esent", "sf", "vf", "ys"]
+              + ["%s%d" % (n, k) for n in ("gv", "gs", "qe", "oo", "oa", "ob", "arr") for k in range(4)]
               + ["%s%d" % (n, i) for n in ("fw", "dw", "qw") for i in range(6)]
               + ["pp%d" % b for b in range(9)])
 
 ADD, MUL, AND = AluOpType.add, AluOpType.mult, AluOpType.bitwise_and
-COPY = ActivationFunctionType.Copy
+COPY, IDENT = ActivationFunctionType.Copy, ActivationFunctionType.Identity
 
 
 def rank_program(g, core, T, topo):
@@ -54,231 +55,251 @@ def rank_program(g, core, T, topo):
     S = T.sem
     V, A, P, Y = g.vector, g.scalar, g.tensor, g.sync
     ks = sorted((1, 2, 3), key=lambda k: topo.same_plane(topo.chip(core), topo.chip(T.cores[r ^ k])))
-    k1, k2, k3 = ks
-    q1, q2, q3 = [r ^ k for k in ks]
+    qs = [r ^ k for k in ks] + [r]
+    q1, q2, q3 = qs[:3]
     tiles = [{r, q1}, {r, q2}, {r, q3}, {q1, q2}, {q1, q3}, {q2, q3}]
-    dsts = [T.cores[q] for q in (q1, q2, q3)]
+    dsts = [T.cores[q] for q in qs[:3]]
     engs = [e for e in topo.engines(core, dsts[0]) if all(e in topo.engines(core, d) for d in dsts)]
     ne = len(engs)
     mask = sum(1 << e for e in engs)
-    parts = [engs[0::2], engs[1::4], engs[3::4]]
+    halves = [sum(1 << e for e in engs[h::2]) for h in range(2)]
+
+    def zrows(i):
+        if tiles[i] in ({0, 1}, {2, 3}):
+            return slice(64, 128) if 0 in tiles[i] else slice(0, 64)
+        return slice(0, 128)
 
     for s in range(4):
         for l in range(2):
             p = 32 * s + 16 * l
-            if s < 3:
-                m = M0[s]
-                Y.dma_start(T.cxy[p:p + 16, 0:C], T.px[:, m:m + C]).then_inc(S.lx, 16)
-                A.dma_start(T.cxy[p:p + 16, C:2 * C], T.py[:, m:m + C]).then_inc(S.ly, 16)
-            else:
-                Y.dma_start(T.cxy[p:p + 16, 0:32], T.px[:]).then_inc(S.lx, 16)
-                A.dma_start(T.cxy[p:p + 16, 32:64], T.py[:]).then_inc(S.ly, 16)
+            m, n = (M0[s], C) if s < 3 else (0, 32)
+            Y.dma_start(T.cxy[p:p + 16, 0, 0:n], T.px[:, m:m + n]).then_inc(S.lx, 16)
+            A.dma_start(T.cxy[p:p + 16, 1, 0:n], T.py[:, m:m + n]).then_inc(S.ly, 16)
     for s in range(4):
-        q = r if s != r else (r + 1) % N
-        Y.dma_start(T.tbl[32 * s:32 * s + 32, :], T.tb[32 * q:32 * q + 32, :]).then_inc(S.tbs, 16)
+        if s != r:
+            Y.dma_start(T.tbl[32 * s:32 * s + 32, :], T.tb[32 * r:32 * r + 32, :]).then_inc(S.tbs, 16)
 
     def wload(i, n):
-        Y.wait_ge(S["fw%d" % i], n)
+        if zrows(i) == slice(0, 128):
+            Y.wait_ge(S["fw%d" % i], n)
         a, b = sorted(tiles[i])
         for q, s in ((a, b), (b, a)):
             Y.dma_start(T["wt%d" % i][32 * s:32 * s + 32, :], T.w[32 * q:32 * q + 32, :]).then_inc(S["dw%d" % i], 16)
 
-    wload(0, 1)
-    wload(2, 3)
-    wload(1, 2)
-    Y.wait_ge(S.lsent, ne)
-    for i, n in ((3, 3), (4, 3), (5, 1)):
-        wload(i, n)
+    fills = {0: 1, 1: 1, 2: 1, 3: 3, 4: 1, 5: 3}
+    for i in (0, 5, 1):
+        wload(i, fills[i])
+    Y.wait_ge(S.lsent, ne + ne)
+    for i in (2, 4, 3):
+        wload(i, fills[i])
 
-    g.iota(T.pw[:], [[0, 16]], 0, 1).then_inc(S.iot, 1)
-    trs = []
-    for k, q, d, es in zip(ks, (q1, q2, q3), dsts, parts):
-        rid, pid, _ = topo.addr(d)
-        trs.append(RemoteDMATransfer(
-            dst_ids=[DstId(rid=rid, pnc=pid)], dma_engine_mask=sum(1 << e for e in es), remote_sem=S.larr,
-            srcs=[T.lout[:, 12 * q:12 * q + 12]], dsts=[T.lin[:, 12 * k:12 * k + 12]]))
-    g.wait_ge(S.lo, 3)
-    g.remote_dma_fused(trs, local_sem=S.lsent)
-    for k, d in zip(ks, dsts):
-        rid, pid, _ = topo.addr(d)
-        g.wait_ge(S["qe%d" % k], 1)
-        g.remote_dma(T["rq%d" % k][:].bitcast(dt.uint8), T["eq%d" % k][:].bitcast(dt.uint8), S["arr%d" % k], S.esent, pid, rid, mask)
-        g.remote_dma(T["rs%d" % k][:], T["es%d" % k][:], S["arr%d" % k], S.esent, pid, rid, mask)
+    g.iota(T.pw[:, 0:12], [[0, 12]], 0, 1).then_inc(S.iot, 1)
+    g.iota(T.pw[:, 12:16], [[-32, 4]], 0, 1).then_inc(S.iot, 1)
+    adr = [topo.addr(d) for d in dsts]
+    g.wait_ge(S.loa, 1)
+    g.remote_dma(T.lin[:, 0:12], T.lout[:, 0:12], S.laa, S.lsent, adr[0][1], adr[0][0], mask)
+    g.wait_ge(S.lob, 1)
+    g.remote_dma_fused([RemoteDMATransfer(
+        dst_ids=[DstId(rid=adr[j][0], pnc=adr[j][1])], dma_engine_mask=halves[j - 1], remote_sem=S.lab,
+        srcs=[T.lout[:, 12 * j:12 * j + 12]], dsts=[T.lin[:, 12 * j:12 * j + 12]]) for j in (1, 2)], local_sem=S.lsent)
+    for j in range(3):
+        rid, pid, _ = adr[j]
+        g.wait_ge(S["qe%d" % j], 1)
+        g.remote_dma(T["rq%d" % j][:].bitcast(dt.uint8), T["eq%d" % j][:].bitcast(dt.uint8), S["arr%d" % j], S.esent, pid, rid, mask)
+        g.remote_dma(T["rs%d" % j][:], T["es%d" % j][:], S["arr%d" % j], S.esent, pid, rid, mask)
     g.wait_ge(S.esent, 6 * ne)
 
+    def vfill(i):
+        V.memset(T["wt%d" % i][zrows(i), :], 0.0).then_inc(S["fw%d" % i], 1)
+
     V.memset(T.zb[:], 0.0).then_inc(S.fz, 1)
-    V.memset(T.wt0[:], 0.0).then_inc(S.fw0, 1)
-    V.memset(T.lout[:], 0).then_inc(S.cd, 1)
-    V.memset(T.xs[96:128, :], 0).then_inc(S.cd, 1)
-    V.wait_ge(S.iot, 1)
-    V.tensor_scalar(T.lw[:], T.pw[:], 16, None, AND).then_inc(S.ct, 1)
-    V.wait_ge(S.ct, 1)
-    for q in range(N):
-        a, b = 2 * q, 2 * q + 1
-        V.tensor_scalar(T.sc[:, q:q + 1], T.lw[:, 0:1], 2.0 ** -SH[a] / 16.0, 2.0 ** -SH[a], MUL, ADD).then_inc(S.cd, 1)
-        for c, M in ((0, MA), (4 * C, MB)):
-            V.tensor_scalar(T.ab[:, c + q:c + 4 * C:4], T.lw[:, 0:C], (M[b] - M[a]) / 4.0, 4.0 * M[a], MUL, ADD).then_inc(S.cd, 1)
-    V.wait_ge(S.cd, 14)
-    V.tensor_scalar(T.bc[:], T.sc[:], 0.5, -0.5, MUL, ADD).then_inc(S.cd, 1)
-    V.memset(T.wt1[:, 0:512], 0.0).then_inc(S.fw1, 1)
-    V.wait_ge(S.cd, 15)
+    V.memset(T.xs[:], 0).then_inc(S.c0, 1)
+    V.wait_ge(S.iot, 2)
+    V.tensor_scalar(T.lw[:], T.pw[:, 0:12], 16, None, AND).then_inc(S.c0, 1)
+    V.tensor_scalar(T.nz[:], T.pw[:, 12:16], 5, None, AluOpType.arith_shift_right).then_inc(S.c0, 1)
+    V.wait_ge(S.c0, 3)
+    V.tensor_scalar(T.lf[:], T.lw[:], 1.0 / 16, 1.0, MUL, ADD).then_inc(S.c1, 1)
+    V.memset(T.tbl[32 * r:32 * r + 32, 0:16], 0.0).then_inc(S.tz, 1)
+    V.wait_ge(S.c1, 1)
+    V.tensor_scalar(T.uf[:], T.nz[:], 0.0, T.lf[:, 0:1], AluOpType.not_equal, MUL).then_inc(S.c2, 1)
+    vfill(1)
+
+    def shift(j, sem):
+        q = qs[j]
+        parts = [(0, 128, 0)] if q == 0 else [(0, 96, 0)] if q == 3 else [(0, 96, 0), (96, 128, M0[q])]
+        for a, b, m in parts:
+            V.tensor_scalar(T.xs[a:b, :, 12 * j:12 * j + C], T.cxy[a:b, :, m:m + C], T.sc[a:b, j:j + 1], T.bc[a:b, j:j + 1], MUL, ADD).then_inc(sem, 1)
+        return len(parts)
+
+    def step(n, c, sem, cnt, done):
+        V.wait_ge(sem, cnt)
+        if n == 0:
+            V.tensor_tensor(T.xm[:, :, c], T.xs[:, :, c], T.ab[:, :, c], MUL).then_inc(sem, 1)
+        elif n == 1:
+            V.tensor_tensor(T.xa[:, c], T.xm[:, 0, c], T.xm[:, 1, c], ADD).then_inc(sem, 1)
+        elif n == 2:
+            V.tensor_scalar(T.adr[:, c], T.xa[:, c], 4 * (K - 1), None, AND).then_inc(sem, 1)
+        else:
+            V.tensor_copy(T.lout[:, c], T.adr[:, c]).then_inc(done, 1)
+
+    ca, cb = slice(0, 12), slice(12, 48)
     V.wait_ge(S.lx, 128)
     V.wait_ge(S.ly, 128)
-    for q in range(N):
-        V.tensor_scalar(T.xs[0:96, q:8 * C:4], T.cxy[0:96, 0:2 * C], T.sc[0:96, q:q + 1], T.bc[0:96, q:q + 1], MUL, ADD).then_inc(S.ad, 1)
-        if q < 3:
-            m = M0[q]
-            for c, x in ((0, m), (4 * C, 32 + m)):
-                V.tensor_scalar(T.xs[96:128, c + q:c + 4 * C:4], T.cxy[96:128, x:x + C], T.sc[96:128, q:q + 1], T.bc[96:128, q:q + 1], MUL, ADD).then_inc(S.ad, 1)
-    V.wait_ge(S.ad, 10)
-    V.tensor_tensor(T.xm[:], T.xs[:], T.ab[:], MUL).then_inc(S.ad, 1)
-    V.wait_ge(S.ad, 11)
-    V.tensor_tensor(T.xa[:], T.xm[:, 0:4 * C], T.xm[:, 4 * C:8 * C], ADD).then_inc(S.ad, 1)
-    V.wait_ge(S.ad, 12)
-    V.tensor_scalar(T.adr[:], T.xa[:], 4 * (K - 1), None, AND).then_inc(S.ad, 1)
-    V.wait_ge(S.ad, 13)
-    for q in (q1, q2, q3, r):
-        V.tensor_copy(T.lout[:, 12 * q:12 * q + C], T.adr[:, q:4 * C:4]).then_inc(S.lown if q == r else S.lo, 1)
-    V.memset(T.wt1[:, 512:1536], 0.0).then_inc(S.fw1, 1)
+    V.wait_ge(S.ka, 2)
+    na = shift(0, S.sa)
+    V.wait_ge(S.kb, 6)
+    nb = shift(1, S.sb)
+    V.wait_ge(S.ma, 2)
+    step(0, ca, S.sa, na, None)
+    nb += shift(2, S.sb)
+    step(1, ca, S.sa, na + 1, None)
+    nb += shift(3, S.sb)
+    step(2, ca, S.sa, na + 2, None)
+    V.wait_ge(S.mb, 6)
+    step(0, cb, S.sb, nb, None)
+    step(3, ca, S.sa, na + 3, S.loa)
+    for n in (1, 2, 3):
+        step(n, cb, S.sb, nb + n, S.lob)
 
-    def offs(t, k):
-        c = 12 * k
-        if t:
-            return T["off%d" % t][:, c:c + C]
-        return T.lin[:, c:c + C] if k else T.lout[:, 12 * r:12 * r + C]
+    def offs(t, j):
+        b = T["off%d" % t] if t else T.lin if j < 3 else T.lout
+        return b[:, 12 * j:12 * j + C]
 
-    V.wait_ge(S.lown, 1)
-    for t in (3, 1, 2):
-        V.tensor_scalar(T["off%d" % t][:, 0:12], T.lout[:, 12 * r:12 * r + 12], float(t), None, ADD).then_inc(S["oo%d" % t], 1)
+    def vo(src, c, sem):
+        for t in (3, 1, 2):
+            V.tensor_scalar(T["off%d" % t][:, c], src[:, c], float(t), None, ADD).then_inc(S[sem % t], 1)
 
-    def vg(k):
+    def vg(j):
         for t in (1, 2):
-            V.tensor_copy(T["eb%d" % k][:, t:4 * NC:4], T.tbl[:].indirect(offs(t, k))).then_inc(S["gv%d" % k], 1)
+            V.tensor_copy(T["eb%d" % j][:, t:4 * NC:4], T.tbl[:].indirect(offs(t, j))).then_inc(S["gv%d" % j], 1)
 
-    def vq(k):
-        if k:
-            V.wait_ge(S["gv%d" % k], 2)
-        V.wait_ge(S["gs%d" % k], 2 if k else 4)
-        V.quantize_mx(T["eq%d" % k][:], T["es%d" % k][:], T["eb%d" % k][:]).then_inc(S["qe%d" % k], 1)
+    def vq(j):
+        if j < 3:
+            V.wait_ge(S["gv%d" % j], 2)
+        V.wait_ge(S["gs%d" % j], 2 if j < 3 else 4)
+        V.quantize_mx(T["eq%d" % j][:], T["es%d" % j][:], T["eb%d" % j][:]).then_inc(S["qe%d" % j], 1)
 
     def vw(i):
+        V.wait_ge(S["fw%d" % i], fills[i])
         V.wait_ge(S["dw%d" % i], 32)
         V.quantize_mx(T["wq%d" % i][:], T["ws%d" % i][:], T["wt%d" % i][:]).then_inc(S["qw%d" % i], 1)
 
-    vw(0)
-    vw(2)
-    V.memset(T.wt5[:], 0.0).then_inc(S.fw5, 1)
+    V.wait_ge(S.lob, 1)
+    vo(T.lout, slice(36, 48), "oo%d")
+    vfill(2)
+    vfill(4)
+    vfill(0)
+    V.wait_ge(S.tbs, 48)
+    V.wait_ge(S.tz, 1)
+    V.wait_ge(S.laa, ne)
+    vo(T.lin, ca, "oa%d")
+    V.wait_ge(S.oa1, 1)
+    V.wait_ge(S.oa2, 1)
+    vg(0)
+    V.wait_ge(S.lab, ne)
+    vo(T.lin, slice(12, 36), "ob%d")
     vq(0)
-    vw(1)
-    V.wait_ge(S.tbs, 64)
-    V.wait_ge(S.larr, ne)
-    for t in (3, 1, 2):
-        V.tensor_scalar(T["off%d" % t][:, 12:48], T.lin[:, 12:48], float(t), None, ADD).then_inc(S["oi%d" % t], 1)
-    V.wait_ge(S.oi1, 1)
-    V.wait_ge(S.oi2, 1)
-    for k in ks:
-        vg(k)
-        vq(k)
-    for i in (3, 4, 5):
+    V.wait_ge(S.ob1, 1)
+    V.wait_ge(S.ob2, 1)
+    for j in (1, 2):
+        vg(j)
+        vq(j)
+    vq(3)
+    for i in (0, 1, 2, 3, 4, 5):
         vw(i)
 
+    def const(j):
+        q = qs[j]
+        f = 2.0 ** -SH[2 * q]
+        A.activation(T.sc[:, j:j + 1], T.uf[:, q:q + 1], IDENT, scale=f).then_inc(S.kb if j else S.ka, 1)
+        A.activation(T.bc[:, j:j + 1], T.uf[:, q:q + 1], IDENT, bias=-0.5, scale=f / 2).then_inc(S.kb if j else S.ka, 1)
+
+    def mult(j):
+        a, b = 2 * qs[j], 2 * qs[j] + 1
+        for c, M in ((0, MA), (1, MB)):
+            A.activation(T.ab[:, c, 12 * j:12 * j + 12], T.lf[:], IDENT, bias=4.0 * (2 * M[a] - M[b]), scale=4.0 * (M[b] - M[a])).then_inc(S.mb if j else S.ma, 1)
+
+    def afill(i, c):
+        A.activation(T["wt%d" % i][zrows(i), c:c + 512], T.zb[zrows(i), :], COPY).then_inc(S["fw%d" % i], 1)
+
+    def ag(j, t):
+        A.activation(T["eb%d" % j][:, t:4 * NC:4], T.tbl[:].indirect(offs(t, j)), COPY).then_inc(S["gs%d" % j], 1)
+
+    A.wait_ge(S.c1, 1)
+    mult(0)
+    A.wait_ge(S.c2, 1)
+    for j in range(4):
+        const(j)
+    for j in (1, 2, 3):
+        mult(j)
     A.wait_ge(S.fz, 1)
-    for i in (2, 3, 4):
-        for c in range(0, 1536, 512):
-            A.activation(T["wt%d" % i][:, c:c + 512], T.zb[:], COPY).then_inc(S["fw%d" % i], 1)
-    A.wait_ge(S.tbs, 64)
-
-    def ag(k, t):
-        A.activation(T["eb%d" % k][:, t:4 * NC:4], T.tbl[:].indirect(offs(t, k)), COPY).then_inc(S["gs%d" % k], 1)
-
-    A.wait_ge(S.lown, 1)
-    ag(0, 0)
+    afill(3, 0)
+    afill(3, 512)
+    A.wait_ge(S.tbs, 48)
+    A.wait_ge(S.tz, 1)
+    A.wait_ge(S.lob, 1)
+    ag(3, 0)
     for t in (3, 1, 2):
         A.wait_ge(S["oo%d" % t], 1)
-        ag(0, t)
-    A.wait_ge(S.larr, ne)
-    for n, k in enumerate(ks):
-        ag(k, 0)
-        if n == 0:
-            A.wait_ge(S.oi3, 1)
-        ag(k, 3)
+        ag(3, t)
+    afill(3, 1024)
+    A.wait_ge(S.laa, ne)
+    ag(0, 0)
+    A.wait_ge(S.oa3, 1)
+    ag(0, 3)
+    A.wait_ge(S.lab, ne)
+    ag(1, 0)
+    A.wait_ge(S.ob3, 1)
+    ag(1, 3)
+    ag(2, 0)
+    ag(2, 3)
+    for c in (0, 512, 1024):
+        afill(5, c)
 
-    seq = [(0, 2), (0, 0), (0, 1), (1, 0), (1, 2), (1, 1), (2, 0), (2, 1), (2, 2)]
-    pas = [(0, 2), (1, 2)]
-    keep = [x for x in seq if x not in pas]
+    seq = [(o, th) for o in range(O) for th in range(3)]
+    lo = (0, 0, 16 * (M0[1] + C - M0[2]))
+    seen, begun = [], []
 
-    def base(x):
-        return 512 * (7 if x in pas else keep.index(x))
+    def third(j, i):
+        s = min(tiles[i] - {qs[j]})
+        return s if s < 3 else qs[j]
 
-    seen = []
-
-    def mm(k, x, first, last):
-        e, z = ("rq%d", "rs%d") if k else ("eq%d", "es%d")
-        o, th = x
-        q = r ^ k
-        s = 3 if (th == q and q < 3) else th
-        i = tiles.index({q, s})
-        if i not in seen:
-            seen.append(i)
-            P.wait_ge(S["qw%d" % i], 1)
+    def mm(j, i, o, last):
+        e, z = ("rq%d", "rs%d") if j < 3 else ("eq%d", "es%d")
+        for sem, cnt in (("qw%d" % i, 1), ("arr%d" % j, 2 * ne) if j < 3 else ("qe3", 1)):
+            if sem not in seen:
+                seen.append(sem)
+                P.wait_ge(S[sem], cnt)
+        th = third(j, i)
+        n = seq.index((o, th))
+        first = n not in begun
+        begun.append(n)
         c = slice(128 * o, 128 * o + 128)
-        b = base(x)
-        return P.matmul_mx(T.acc[:, b:b + NC], T["wq%d" % i][:, c], T["ws%d" % i][:, c], T[e % k][:], T[z % k][:], first, last)
+        b = 512 * (n % 8)
+        return P.matmul_mx(T.acc[:, b:b + NC - lo[th]], T["wq%d" % i][:, c], T["ws%d" % i][:, c],
+                           T[e % j][:, lo[th]:NC], T[z % j][:, lo[th]:NC], first, last)
 
-    P.wait_ge(S.qe0, 1)
-    for x in seq:
-        if x in pas:
-            if x == pas[1]:
-                P.wait_ge(S.rv, 1)
-            mm(0, x, True, True).then_inc(S.pr, 1)
-        else:
-            mm(0, x, True, False)
-    P.wait_ge(S["arr%d" % k1], 2 * ne)
-    for x in keep:
-        mm(k1, x, False, False)
-    P.wait_ge(S["arr%d" % k2], 2 * ne)
-    for x in seq:
-        if x in pas:
-            if x == pas[0]:
-                P.wait_ge(S.rv, 2)
-            else:
-                P.wait_ge(S.vb, 1)
-            mm(k1, x, True, False)
-            mm(k2, x, False, True).then_inc(S.pb, 1)
-        else:
-            mm(k2, x, False, False)
-    P.wait_ge(S["arr%d" % k3], 2 * ne)
-    for n, x in enumerate(seq):
-        if x in pas:
-            if x == pas[0]:
-                P.wait_ge(S.vb, 2)
-            else:
-                P.wait_ge(S.vf, 1)
-        mm(k3, x, x in pas, True).then_inc(S["pp%d" % n], 1)
+    for j, i in ((3, 0), (0, 0), (3, 1), (3, 2), (0, 3), (1, 1), (1, 3), (0, 4), (1, 5)):
+        for o in range(O):
+            if (o, third(j, i)) != seq[8]:
+                mm(j, i, o, False)
 
-    for i in range(2):
-        A.wait_ge(S.pr, i + 1)
-        A.activation(T.part[:, NC * i:NC * i + NC], T.acc[:, 3584:3584 + NC], COPY).then_inc(S.rv, 1)
-    for i in range(2):
-        pi = T.part[:, NC * i:NC * i + NC]
-        V.wait_ge(S.pb, i + 1)
-        V.wait_ge(S.rv, i + 1)
-        V.tensor_tensor(pi, T.acc[:, 3584:3584 + NC], pi, ADD).then_inc(S.vb, 1)
+    def tile_of(j, th):
+        return [i for i in range(6) if qs[j] in tiles[i] and third(j, i) == th][0]
+
+    for n, (o, th) in enumerate(seq[:8]):
+        mm(2, tile_of(2, th), o, True).then_inc(S["pp%d" % n], 1)
+    P.wait_ge(S.vf, 1)
+    for j in (3, 0, 1, 2):
+        m = mm(j, tile_of(j, 2), O - 1, j == 2)
+    m.then_inc(S.pp8, 1)
+
     cnt = {"s": 0, "v": 0}
     done = {}
-    for n, x in enumerate(seq):
-        o, th = x
-        lo = 0 if th < 2 else 16 * (M0[1] + C - M0[2])
-        y = T.yb[:, 512 * o + 16 * M0[th] + lo:512 * o + 16 * M0[th] + NC]
-        b = base(x)
-        a = T.acc[:, b + lo:b + NC]
-        if x in pas:
-            i = pas.index(x)
-            V.wait_ge(S["pp%d" % n], 1)
-            V.wait_ge(S.vb, i + 1)
-            V.tensor_tensor(y, a, T.part[:, NC * i + lo:NC * i + NC], ADD).then_inc(S.vf, 1)
-            cnt["v"] += 1
-        elif n % 2:
+    for n, (o, th) in enumerate(seq):
+        y = T.yb[:, 512 * o + 16 * M0[th] + lo[th]:512 * o + 16 * M0[th] + NC]
+        a = T.acc[:, 512 * (n % 8):512 * (n % 8) + NC - lo[th]]
+        if n % 2:
             A.wait_ge(S["pp%d" % n], 1)
             A.activation(y, a, COPY).then_inc(S.sf, 1)
             cnt["s"] += 1

@@ -14,18 +14,15 @@ F8 = "float8_e4m3fn_x4"
 
 SCRATCH = {
     "cxy": ("sbuf", [128, 2, 32], "int32"),
-    "pw": ("sbuf", [128, 16], "int32"), "lw": ("sbuf", [128, 12], "int32"), "nz": ("sbuf", [128, 4], "int32"),
-    "lf": ("sbuf", [128, 12], "float32"), "uf": ("sbuf", [128, 4], "float32"),
-    "ab": ("sbuf", [128, 2, 48], "float32"), "sc": ("sbuf", [128, 4], "float32"), "bc": ("sbuf", [128, 4], "float32"),
+    "pw": ("sbuf", [128, 12], "int32"), "lw": ("sbuf", [128, 12], "int32"), "lf": ("sbuf", [128, 12], "float32"),
+    "ab": ("sbuf", [128, 2, 48], "float32"), "sc": ("sbuf", [128, 4], "float32"),
     "xs": ("sbuf", [128, 2, 48], "int32"), "xm": ("sbuf", [128, 2, 48], "float32"),
     "xa": ("sbuf", [128, 48], "int32"), "adr": ("sbuf", [128, 48], "int32"),
     "lout": ("sbuf", [128, 48], "uint16"), "lin": ("sbuf", [128, 48], "uint16"),
-    "tbl": ("sbuf", [128, 4 * K], "bfloat16"), "zb": ("sbuf", [128, 512], "bfloat16"),
-    "yb": ("sbuf", [128, 1536], "float32"),
+    "tbl": ("sbuf", [128, 4 * K], "bfloat16"), "tbp": ("sbuf", [128, 4 * K], "bfloat16"), "zb": ("sbuf", [128, 768], "bfloat16"),
+    "yb": ("sbuf", [128, 1536], "float32"), "part": ("sbuf", [128, NC], "float32"),
     "acc": ("psum", [128, 4096], "float32"),
 }
-for _t in (1, 2, 3):
-    SCRATCH["off%d" % _t] = ("sbuf", [128, 48], "uint16")
 for _i in range(6):
     SCRATCH["wt%d" % _i] = ("sbuf", [128, 1536], "bfloat16")
     SCRATCH["wq%d" % _i] = ("sbuf", [128, 384], F8)
@@ -38,11 +35,17 @@ for _j in range(4):
         SCRATCH["rq%d" % _j] = ("sbuf", [128, NC], F8)
         SCRATCH["rs%d" % _j] = ("sbuf", [128, NC], "uint8")
 
-SEMAPHORES = (["lx", "ly", "fz", "tz", "tbs", "iot", "c0", "c1", "c2", "ka", "kb", "ma", "mb", "sa", "sb", "loa", "lob",
-               "laa", "lab", "lsent", "esent", "sf", "vf", "ys"]
-              + ["%s%d" % (n, k) for n in ("gv", "gs", "qe", "oo", "oa", "ob", "arr") for k in range(4)]
+SEMAPHORES = (["la", "lb", "fz", "tbs", "iot", "c0", "c1", "ka", "ma", "mb", "sa", "sb", "loa", "lob",
+               "laa", "lab", "lsent", "esent", "sf", "vf", "ys", "pa", "pb"]
+              + ["%s%d" % (n, k) for n in ("gv", "gs", "qe", "pl", "arr") for k in range(4)]
               + ["%s%d" % (n, i) for n in ("fw", "dw", "qw") for i in range(6)]
               + ["pp%d" % b for b in range(9)])
+
+YPLAN = "w0 z0 w4 z4 w1 l0 w3 w2 w5"
+VPLAN = "f1012 s0 f13 a0 s1 s2 a1 s3 a2 b0 a3 b1 f20 b2 f21 b3 d1 d2 d3 f223 w0 w1 g00 g01 q3 q0 g10 g11 g20 q1 w3 q2 w4 w2 w5"
+APLAN = "f301 f323 d0 g30 g31 g32 g33 g02 g03 g12 g13 g21 g22 g23 p00 f501 f523"
+PPLAN = "30 31 00 03 04 32 11 13 15"
+STORES = "0 12 345 678"
 
 ADD, MUL, AND = AluOpType.add, AluOpType.mult, AluOpType.bitwise_and
 COPY, IDENT = ActivationFunctionType.Copy, ActivationFunctionType.Identity
@@ -64,37 +67,63 @@ def rank_program(g, core, T, topo):
     mask = sum(1 << e for e in engs)
     halves = [sum(1 << e for e in engs[h::2]) for h in range(2)]
 
+    lo = (0, 0, 16 * (M0[1] + C - M0[2]))
+
+    def third(j, i):
+        s = min(tiles[i] - {qs[j]})
+        return s if s < 3 else qs[j]
+
+    def tile_of(j, th):
+        return [i for i in range(6) if qs[j] in tiles[i] and third(j, i) == th][0]
+
+    plan = [(int(x[0]), int(x[1])) for x in PPLAN.split()]
+    own = [third(j, i) for j, i in plan if j == 3]
+    t8 = own[0] if own[0] != 1 else own[1]
+    seq = [(o, th) for o in range(O - 1) for th in range(3)] + [(O - 1, th) for th in (own[0] + own[1] - t8, own[2], t8)]
+    met = []
+
+    def once(queue, name, sem, n):
+        if (name, sem) not in met:
+            met.append((name, sem))
+            queue.wait_ge(S[sem], n)
+
     def zrows(i):
         if tiles[i] in ({0, 1}, {2, 3}):
             return slice(64, 128) if 0 in tiles[i] else slice(0, 64)
         return slice(0, 128)
 
-    for s in range(4):
+    for s in sorted(range(4), key=lambda s: s == q1):
         for l in range(2):
             p = 32 * s + 16 * l
             m, n = (M0[s], C) if s < 3 else (0, 32)
-            Y.dma_start(T.cxy[p:p + 16, 0, 0:n], T.px[:, m:m + n]).then_inc(S.lx, 16)
-            A.dma_start(T.cxy[p:p + 16, 1, 0:n], T.py[:, m:m + n]).then_inc(S.ly, 16)
+            Y.dma_start(T.cxy[p:p + 16, 0, 0:n], T.px[:, m:m + n]).then_inc(S.lb if s == q1 else S.la, 16)
+            A.dma_start(T.cxy[p:p + 16, 1, 0:n], T.py[:, m:m + n]).then_inc(S.lb if s == q1 else S.la, 16)
     for s in range(4):
-        if s != r:
-            Y.dma_start(T.tbl[32 * s:32 * s + 32, :], T.tb[32 * r:32 * r + 32, :]).then_inc(S.tbs, 16)
+        q = r if s != r else (r + 1) % N
+        (Y, A)[s % 2].dma_start(T.tbl[32 * s:32 * s + 32, :], T.tb[32 * q:32 * q + 32, :]).then_inc(S.tbs, 16)
 
-    def wload(i, n):
-        if zrows(i) == slice(0, 128):
-            Y.wait_ge(S["fw%d" % i], n)
-        a, b = sorted(tiles[i])
-        for q, s in ((a, b), (b, a)):
-            Y.dma_start(T["wt%d" % i][32 * s:32 * s + 32, :], T.w[32 * q:32 * q + 32, :]).then_inc(S["dw%d" % i], 16)
+    fills = [i for i in range(6) if "f%d0" % i in VPLAN + APLAN]
+    for x in YPLAN.split():
+        i = int(x[1])
+        if x[0] == "w":
+            if i in fills and zrows(i) == slice(0, 128):
+                Y.wait_ge(S["fw%d" % i], 4)
+            a, b = sorted(tiles[i])
+            for q, s in ((a, b), (b, a)):
+                Y.dma_start(T["wt%d" % i][32 * s:32 * s + 32, :], T.w[32 * q:32 * q + 32, :]).then_inc(S["dw%d" % i], 16)
+        elif x[0] == "z":
+            once(Y, "y", "fz", 1)
+            if zrows(i) != slice(0, 128):
+                Y.dma_start(T["wt%d" % i][zrows(i), :], T.zb[:]).then_inc(S["dw%d" % i], 32)
+                continue
+            for s in sorted(set(range(N)) - tiles[i]):
+                Y.dma_start(T["wt%d" % i][32 * s:32 * s + 32, :], T.zb[0:64, :]).then_inc(S["dw%d" % i], 16)
+        elif x[0] == "l":
+            Y.wait_ge(S.lsent, ne + ne)
+        else:
+            Y.wait_ge(S["qe%d" % i], 1)
 
-    fills = {0: 1, 1: 1, 2: 1, 3: 3, 4: 1, 5: 3}
-    for i in (0, 5, 1):
-        wload(i, fills[i])
-    Y.wait_ge(S.lsent, ne + ne)
-    for i in (2, 4, 3):
-        wload(i, fills[i])
-
-    g.iota(T.pw[:, 0:12], [[0, 12]], 0, 1).then_inc(S.iot, 1)
-    g.iota(T.pw[:, 12:16], [[-32, 4]], 0, 1).then_inc(S.iot, 1)
+    g.iota(T.pw[:], [[0, 12]], 0, 1).then_inc(S.iot, 1)
     adr = [topo.addr(d) for d in dsts]
     g.wait_ge(S.loa, 1)
     g.remote_dma(T.lin[:, 0:12], T.lout[:, 0:12], S.laa, S.lsent, adr[0][1], adr[0][0], mask)
@@ -109,26 +138,23 @@ def rank_program(g, core, T, topo):
         g.remote_dma(T["rs%d" % j][:], T["es%d" % j][:], S["arr%d" % j], S.esent, pid, rid, mask)
     g.wait_ge(S.esent, 6 * ne)
 
-    def vfill(i):
-        V.memset(T["wt%d" % i][zrows(i), :], 0.0).then_inc(S["fw%d" % i], 1)
-
-    V.memset(T.zb[:], 0.0).then_inc(S.fz, 1)
     V.memset(T.xs[:], 0).then_inc(S.c0, 1)
-    V.wait_ge(S.iot, 2)
-    V.tensor_scalar(T.lw[:], T.pw[:, 0:12], 16, None, AND).then_inc(S.c0, 1)
-    V.tensor_scalar(T.nz[:], T.pw[:, 12:16], 5, None, AluOpType.arith_shift_right).then_inc(S.c0, 1)
-    V.wait_ge(S.c0, 3)
-    V.tensor_scalar(T.lf[:], T.lw[:], 1.0 / 16, 1.0, MUL, ADD).then_inc(S.c1, 1)
-    V.memset(T.tbl[32 * r:32 * r + 32, 0:16], 0.0).then_inc(S.tz, 1)
-    V.wait_ge(S.c1, 1)
-    V.tensor_scalar(T.uf[:], T.nz[:], 0.0, T.lf[:, 0:1], AluOpType.not_equal, MUL).then_inc(S.c2, 1)
-    vfill(1)
+    V.memset(T.zb[:], 0.0).then_inc(S.fz, 1)
+    V.wait_ge(S.iot, 1)
+    V.tensor_scalar(T.lw[:], T.pw[:], 16, None, AND).then_inc(S.c0, 1)
+    V.wait_ge(S.c0, 2)
+    V.tensor_copy(T.lf[:], T.lw[:]).then_inc(S.c1, 1)
+    for j in range(4):
+        f = 2.0 ** -SH[2 * qs[j]]
+        V.tensor_scalar(T.sc[:, j:j + 1], T.lw[:, 0:1], f / 16, f, MUL, ADD).then_inc(S.ka, 1)
 
     def shift(j, sem):
         q = qs[j]
         parts = [(0, 128, 0)] if q == 0 else [(0, 96, 0)] if q == 3 else [(0, 96, 0), (96, 128, M0[q])]
+        if j == 0 and q < 3:
+            parts = [[(32, 64, 0), (64, 128, 0)], [(0, 32, 0), (64, 96, 0), parts[-1]], [(0, 64, 0), parts[-1]]][q]
         for a, b, m in parts:
-            V.tensor_scalar(T.xs[a:b, :, 12 * j:12 * j + C], T.cxy[a:b, :, m:m + C], T.sc[a:b, j:j + 1], T.bc[a:b, j:j + 1], MUL, ADD).then_inc(sem, 1)
+            V.tensor_scalar(T.xs[a:b, :, 12 * j:12 * j + C], T.cxy[a:b, :, m:m + C], T.sc[a:b, j:j + 1], 2.0 ** -8 - 0.5, MUL, ADD).then_inc(sem, 1)
         return len(parts)
 
     def step(n, c, sem, cnt, done):
@@ -138,178 +164,133 @@ def rank_program(g, core, T, topo):
         elif n == 1:
             V.tensor_tensor(T.xa[:, c], T.xm[:, 0, c], T.xm[:, 1, c], ADD).then_inc(sem, 1)
         elif n == 2:
-            V.tensor_scalar(T.adr[:, c], T.xa[:, c], 4 * (K - 1), None, AND).then_inc(sem, 1)
+            V.tensor_scalar(T.adr[:, c], T.xa[:, c], K - 1, None, AND).then_inc(sem, 1)
         else:
             V.tensor_copy(T.lout[:, c], T.adr[:, c]).then_inc(done, 1)
 
-    ca, cb = slice(0, 12), slice(12, 48)
-    V.wait_ge(S.lx, 128)
-    V.wait_ge(S.ly, 128)
-    V.wait_ge(S.ka, 2)
-    na = shift(0, S.sa)
-    V.wait_ge(S.kb, 6)
-    nb = shift(1, S.sb)
-    V.wait_ge(S.ma, 2)
-    step(0, ca, S.sa, na, None)
-    nb += shift(2, S.sb)
-    step(1, ca, S.sa, na + 1, None)
-    nb += shift(3, S.sb)
-    step(2, ca, S.sa, na + 2, None)
-    V.wait_ge(S.mb, 6)
-    step(0, cb, S.sb, nb, None)
-    step(3, ca, S.sa, na + 3, S.loa)
-    for n in (1, 2, 3):
-        step(n, cb, S.sb, nb + n, S.lob)
+    made = {"a": 0, "b": 0}
 
-    def offs(t, j):
-        b = T["off%d" % t] if t else T.lin if j < 3 else T.lout
-        return b[:, 12 * j:12 * j + C]
+    def addresses(x, n):
+        if x == "s":
+            once(V, "v", "ka", 4)
+            once(V, "v", "lb" if n else "la", 64 if n else 192)
+            made["b" if n else "a"] += shift(n, S.sb if n else S.sa)
+        elif x == "a":
+            once(V, "v", "ma", 2)
+            step(n, slice(0, 12), S.sa, made[x] + n, S.loa)
+        else:
+            once(V, "v", "mb", 6)
+            step(n, slice(12, 48), S.sb, made[x] + n, S.lob)
 
-    def vo(src, c, sem):
-        for t in (3, 1, 2):
-            V.tensor_scalar(T["off%d" % t][:, c], src[:, c], float(t), None, ADD).then_inc(S[sem % t], 1)
+    lists = (("laa", ne), ("lab", ne), ("lab", ne), ("lob", 1))
+    cnt = {e: [plans.count("g%d" % j) for j in range(4)] for e, plans in (("v", VPLAN), ("a", APLAN))}
 
-    def vg(j):
-        for t in (1, 2):
-            V.tensor_copy(T["eb%d" % j][:, t:4 * NC:4], T.tbl[:].indirect(offs(t, j))).then_inc(S["gv%d" % j], 1)
+    def call(Q, name, x):
+        i, t = int(x[1]), int(x[-1])
+        copy = V.tensor_copy if name == "v" else lambda out, in_: A.activation(out, in_, COPY)
+        if x[0] == "f":
+            a, n = int(x[2]), len(x) - 2
+            out = T["wt%d" % i][zrows(i), 384 * a:384 * (a + n)]
+            if name == "v":
+                V.memset(out, 0.0).then_inc(S["fw%d" % i], n)
+            else:
+                once(A, name, "fz", 1)
+                copy(out, T.zb[zrows(i), 0:384 * n]).then_inc(S["fw%d" % i], n)
+        elif x[0] == "d":
+            once(Q, name, "tbs", 64)
+            copy(T.tbp[:, K * t:K * t + K], T.tbl[:, t:4 * K:4]).then_inc(S["pl%d" % t], 1)
+        elif x[0] == "g":
+            once(Q, name, "pl%d" % t, 1)
+            once(Q, name, *lists[i])
+            off = (T.lin if i < 3 else T.lout)[:, 12 * i:12 * i + C]
+            copy(T["eb%d" % i][:, t:4 * NC:4], T.tbp[:, K * t:K * t + K].indirect(off)).then_inc(S[("gv%d" if name == "v" else "gs%d") % i], 1)
+        elif x[0] == "q":
+            for e, sem in (("a", "gs%d"), ("v", "gv%d")):
+                if cnt[e][i]:
+                    V.wait_ge(S[sem % i], cnt[e][i])
+            V.quantize_mx(T["eq%d" % i][:], T["es%d" % i][:], T["eb%d" % i][:]).then_inc(S["qe%d" % i], 1)
+        elif x[0] == "w":
+            if i in fills:
+                V.wait_ge(S["fw%d" % i], 4)
+            V.wait_ge(S["dw%d" % i], 32 if i in fills else 64)
+            V.quantize_mx(T["wq%d" % i][:], T["ws%d" % i][:], T["wt%d" % i][:]).then_inc(S["qw%d" % i], 1)
+        elif x[0] == "p":
+            A.wait_ge(S.pa, 1)
+            copy(T.part[:, 0:NC - lo[t8]], T.acc[:, 3584:3584 + NC - lo[t8]]).then_inc(S.pb, 1)
+        else:
+            addresses(x[0], i)
 
-    def vq(j):
-        if j < 3:
-            V.wait_ge(S["gv%d" % j], 2)
-        V.wait_ge(S["gs%d" % j], 2 if j < 3 else 4)
-        V.quantize_mx(T["eq%d" % j][:], T["es%d" % j][:], T["eb%d" % j][:]).then_inc(S["qe%d" % j], 1)
-
-    def vw(i):
-        V.wait_ge(S["fw%d" % i], fills[i])
-        V.wait_ge(S["dw%d" % i], 32)
-        V.quantize_mx(T["wq%d" % i][:], T["ws%d" % i][:], T["wt%d" % i][:]).then_inc(S["qw%d" % i], 1)
-
-    V.wait_ge(S.lob, 1)
-    vo(T.lout, slice(36, 48), "oo%d")
-    vfill(2)
-    vfill(4)
-    vfill(0)
-    V.wait_ge(S.tbs, 48)
-    V.wait_ge(S.tz, 1)
-    V.wait_ge(S.laa, ne)
-    vo(T.lin, ca, "oa%d")
-    V.wait_ge(S.oa1, 1)
-    V.wait_ge(S.oa2, 1)
-    vg(0)
-    V.wait_ge(S.lab, ne)
-    vo(T.lin, slice(12, 36), "ob%d")
-    vq(0)
-    V.wait_ge(S.ob1, 1)
-    V.wait_ge(S.ob2, 1)
-    for j in (1, 2):
-        vg(j)
-        vq(j)
-    vq(3)
-    for i in (0, 1, 2, 3, 4, 5):
-        vw(i)
-
-    def const(j):
-        q = qs[j]
-        f = 2.0 ** -SH[2 * q]
-        A.activation(T.sc[:, j:j + 1], T.uf[:, q:q + 1], IDENT, scale=f).then_inc(S.kb if j else S.ka, 1)
-        A.activation(T.bc[:, j:j + 1], T.uf[:, q:q + 1], IDENT, bias=-0.5, scale=f / 2).then_inc(S.kb if j else S.ka, 1)
-
-    def mult(j):
-        a, b = 2 * qs[j], 2 * qs[j] + 1
-        for c, M in ((0, MA), (1, MB)):
-            A.activation(T.ab[:, c, 12 * j:12 * j + 12], T.lf[:], IDENT, bias=4.0 * (2 * M[a] - M[b]), scale=4.0 * (M[b] - M[a])).then_inc(S.mb if j else S.ma, 1)
-
-    def afill(i, c):
-        A.activation(T["wt%d" % i][zrows(i), c:c + 512], T.zb[zrows(i), :], COPY).then_inc(S["fw%d" % i], 1)
-
-    def ag(j, t):
-        A.activation(T["eb%d" % j][:, t:4 * NC:4], T.tbl[:].indirect(offs(t, j)), COPY).then_inc(S["gs%d" % j], 1)
+    for x in VPLAN.split():
+        call(V, "v", x)
 
     A.wait_ge(S.c1, 1)
-    mult(0)
-    A.wait_ge(S.c2, 1)
     for j in range(4):
-        const(j)
-    for j in (1, 2, 3):
-        mult(j)
-    A.wait_ge(S.fz, 1)
-    afill(3, 0)
-    afill(3, 512)
-    A.wait_ge(S.tbs, 48)
-    A.wait_ge(S.tz, 1)
-    A.wait_ge(S.lob, 1)
-    ag(3, 0)
-    for t in (3, 1, 2):
-        A.wait_ge(S["oo%d" % t], 1)
-        ag(3, t)
-    afill(3, 1024)
-    A.wait_ge(S.laa, ne)
-    ag(0, 0)
-    A.wait_ge(S.oa3, 1)
-    ag(0, 3)
-    A.wait_ge(S.lab, ne)
-    ag(1, 0)
-    A.wait_ge(S.ob3, 1)
-    ag(1, 3)
-    ag(2, 0)
-    ag(2, 3)
-    for c in (0, 512, 1024):
-        afill(5, c)
+        a, b = 2 * qs[j], 2 * qs[j] + 1
+        for c, M in ((0, MA), (1, MB)):
+            A.activation(T.ab[:, c, 12 * j:12 * j + 12], T.lf[:], IDENT, bias=float(M[a]), scale=(M[b] - M[a]) / 16.0).then_inc(S.mb if j else S.ma, 1)
+    for x in APLAN.split():
+        call(A, "a", x)
 
-    seq = [(o, th) for o in range(O) for th in range(3)]
-    lo = (0, 0, 16 * (M0[1] + C - M0[2]))
-    seen, begun = [], []
-
-    def third(j, i):
-        s = min(tiles[i] - {qs[j]})
-        return s if s < 3 else qs[j]
+    begun = []
 
     def mm(j, i, o, last):
         e, z = ("rq%d", "rs%d") if j < 3 else ("eq%d", "es%d")
-        for sem, cnt in (("qw%d" % i, 1), ("arr%d" % j, 2 * ne) if j < 3 else ("qe3", 1)):
-            if sem not in seen:
-                seen.append(sem)
-                P.wait_ge(S[sem], cnt)
+        once(P, "p", "qw%d" % i, 1)
+        once(P, "p", "arr%d" % j if j < 3 else "qe3", 2 * ne if j < 3 else 1)
         th = third(j, i)
         n = seq.index((o, th))
-        first = n not in begun
+        first = n not in begun or (n, j) == (8, 0)
+        if first and n == 7:
+            P.wait_ge(S.pb, 1)
         begun.append(n)
         c = slice(128 * o, 128 * o + 128)
-        b = 512 * (n % 8)
+        b = 512 * (n if n < 8 else 7 if j == 3 else 0)
         return P.matmul_mx(T.acc[:, b:b + NC - lo[th]], T["wq%d" % i][:, c], T["ws%d" % i][:, c],
                            T[e % j][:, lo[th]:NC], T[z % j][:, lo[th]:NC], first, last)
 
-    for j, i in ((3, 0), (0, 0), (3, 1), (3, 2), (0, 3), (1, 1), (1, 3), (0, 4), (1, 5)):
+    for j, i in plan:
         for o in range(O):
-            if (o, third(j, i)) != seq[8]:
+            x = (o, third(j, i))
+            if (j, x) == (3, seq[8]):
+                mm(j, i, o, True).then_inc(S.pa, 1)
+            elif x != seq[8]:
                 mm(j, i, o, False)
-
-    def tile_of(j, th):
-        return [i for i in range(6) if qs[j] in tiles[i] and third(j, i) == th][0]
-
-    for n, (o, th) in enumerate(seq[:8]):
-        mm(2, tile_of(2, th), o, True).then_inc(S["pp%d" % n], 1)
-    P.wait_ge(S.vf, 1)
-    for j in (3, 0, 1, 2):
-        m = mm(j, tile_of(j, 2), O - 1, j == 2)
-    m.then_inc(S.pp8, 1)
-
-    cnt = {"s": 0, "v": 0}
-    done = {}
     for n, (o, th) in enumerate(seq):
-        y = T.yb[:, 512 * o + 16 * M0[th] + lo[th]:512 * o + 16 * M0[th] + NC]
+        if n == 8:
+            P.wait_ge(S.vf, 1)
+            for j in (0, 1):
+                mm(j, tile_of(j, th), o, False)
+        mm(2, tile_of(2, th), o, True).then_inc(S["pp%d" % n], 1)
+
+    num = {"sf": 0, "vf": 0}
+    done, cols = [], []
+    for n, (o, th) in enumerate(seq):
+        cols.append((512 * o + 16 * M0[th] + lo[th], 512 * o + 16 * M0[th] + NC))
+        y = T.yb[:, cols[n][0]:cols[n][1]]
         a = T.acc[:, 512 * (n % 8):512 * (n % 8) + NC - lo[th]]
         if n % 2:
             A.wait_ge(S["pp%d" % n], 1)
             A.activation(y, a, COPY).then_inc(S.sf, 1)
-            cnt["s"] += 1
         else:
             V.wait_ge(S["pp%d" % n], 1)
-            V.tensor_copy(y, a).then_inc(S.vf, 1)
-            cnt["v"] += 1
-        done[o] = (cnt["s"], cnt["v"])
-    for o in range(O):
-        Y.wait_ge(S.sf, done[o][0])
-        Y.wait_ge(S.vf, done[o][1])
-        Y.dma_start(T.y[:, 512 * o:512 * o + 512], T.yb[:, 512 * o:512 * o + 512]).then_inc(S.ys, 16)
-    Y.wait_ge(S.ys, 16 * O)
+            if n < 8:
+                V.tensor_copy(y, a).then_inc(S.vf, 1)
+            else:
+                V.wait_ge(S.pb, 1)
+                V.tensor_tensor(y, a, T.part[:, 0:NC - lo[th]], ADD).then_inc(S.vf, 1)
+        num["sf" if n % 2 else "vf"] += 1
+        done.append(dict(num))
+    stores, got = 0, {"sf": 0, "vf": 0}
+    for x in STORES.split():
+        runs = sorted(cols[int(n)] for n in x)
+        for sem, n in done[int(x[-1])].items():
+            if n > got[sem]:
+                Y.wait_ge(S[sem], n)
+                got[sem] = n
+        while runs:
+            a, b = runs.pop(0)
+            while runs and runs[0][0] == b:
+                b = runs.pop(0)[1]
+            Y.dma_start(T.y[:, a:b], T.yb[:, a:b]).then_inc(S.ys, 16)
+            stores += 1
+    Y.wait_ge(S.ys, 16 * stores)

@@ -14,7 +14,8 @@ F8 = "float8_e4m3fn_x4"
 
 SCRATCH = {
     "cxy": ("sbuf", [128, 2, 32], "int32"),
-    "pw": ("sbuf", [128, 12], "int32"), "lw": ("sbuf", [128, 12], "int32"), "lf": ("sbuf", [128, 12], "float32"),
+    "cout": ("sbuf", [128, 2, 12], "uint16"), "cin": ("sbuf", [128, 2, 12], "uint16"),
+    "pw": ("sbuf", [128, 24], "int32"), "lw": ("sbuf", [128, 24], "int32"), "lf": ("sbuf", [128, 24], "float32"),
     "ab": ("sbuf", [128, 2, 48], "float32"), "sc": ("sbuf", [128, 4], "float32"),
     "xs": ("sbuf", [128, 2, 48], "int32"), "xm": ("sbuf", [128, 2, 48], "float32"),
     "xa": ("sbuf", [128, 48], "int32"), "adr": ("sbuf", [128, 48], "int32"),
@@ -36,15 +37,15 @@ for _j in range(4):
         SCRATCH["rs%d" % _j] = ("sbuf", [128, NC], "uint8")
 
 SEMAPHORES = (["la", "lb", "fz", "tbs", "iot", "c0", "c1", "ka", "ma", "mb", "sa", "sb", "loa", "lob",
-               "laa", "lab", "lsent", "esent", "sf", "vf", "ys", "pa", "pb"]
+               "laa", "lab", "lac", "loc", "co", "sr", "csent", "lsent", "esent", "sf", "vf", "ys", "pa", "pb"]
               + ["%s%d" % (n, k) for n in ("gv", "gs", "qe", "pl", "arr") for k in range(4)]
               + ["%s%d" % (n, i) for n in ("fw", "dw", "qw") for i in range(6)]
               + ["pp%d" % b for b in range(9)])
 
-YPLAN = "w0 z0 w4 z4 w1 l0 w3 w2 w5"
-VPLAN = "f1012 s0 f13 a0 s1 s2 a1 s3 a2 b0 a3 b1 f20 b2 f21 b3 d1 d2 d3 f223 w0 w1 g00 g01 q3 q0 g10 g11 g20 q1 w3 q2 w4 w2 w5"
-APLAN = "f301 f323 d0 g30 g31 g32 g33 g02 g03 g12 g13 g21 g22 g23 p00 f501 f523"
-PPLAN = "30 31 00 03 04 32 11 13 15"
+YPLAN = "w0 z0 z40 w1 c0 w3 z41 w4 w5 w20 l0"
+VPLAN = "f101 s0 c0 s1 a0 s3 a1 b0 a2 f12 b1 a3 d1 b2 f13 b3 d2 d3 w0 g30 s2 g00 r0 g01 r1 q3 q0 r2 g10 r3 w1 q1 g20 g21 q2 w3 w2 w4 w5"
+APLAN = "f301 f323 d0 g31 g32 g33 g02 g03 g11 g12 g13 g22 g23 f501 p00 f523"
+PPLAN = "30 31 00 03 32 04 11 13 15"
 STORES = "0 12 345 678"
 
 ADD, MUL, AND = AluOpType.add, AluOpType.mult, AluOpType.bitwise_and
@@ -87,6 +88,15 @@ def rank_program(g, core, T, topo):
             met.append((name, sem))
             queue.wait_ge(S[sem], n)
 
+    blk = (0, 1, 3, 2)
+
+    def parts(j, bare):
+        q = qs[j]
+        last = (96, 128, M0[q % 3])
+        if bare:
+            return [[(32, 64, 0), (64, 128, 0)], [(0, 32, 0), (64, 96, 0), last], [(0, 64, 0), last], [(0, 96, 0)]][q]
+        return [(0, 128, 0)] if q == 0 else [(0, 96, 0)] if q == 3 else [(0, 96, 0), last]
+
     def zrows(i):
         if tiles[i] in ({0, 1}, {2, 3}):
             return slice(64, 128) if 0 in tiles[i] else slice(0, 64)
@@ -102,35 +112,45 @@ def rank_program(g, core, T, topo):
         q = r if s != r else (r + 1) % N
         (Y, A)[s % 2].dma_start(T.tbl[32 * s:32 * s + 32, :], T.tb[32 * q:32 * q + 32, :]).then_inc(S.tbs, 16)
 
-    fills = [i for i in range(6) if "f%d0" % i in VPLAN + APLAN]
+    fills = {i: sum(len(x) - 2 for x in (VPLAN + " " + APLAN).split() if x[:2] == "f%d" % i) for i in range(6) if "f%d0" % i in VPLAN + APLAN}
+    after = {int(x[1]): int(x[2]) for x in YPLAN.split() if x[0] == "w" and len(x) == 3}
+    wt = [T["wt%d" % after.get(i, i)] for i in range(6)]
     for x in YPLAN.split():
         i = int(x[1])
         if x[0] == "w":
             if i in fills and zrows(i) == slice(0, 128):
-                Y.wait_ge(S["fw%d" % i], 4)
+                Y.wait_ge(S["fw%d" % i], fills[i])
+            if i in after:
+                Y.wait_ge(S["qw%d" % after[i]], 1)
+                s = min(tiles[after[i]] - tiles[i])
+                Y.dma_start(wt[i][32 * s:32 * s + 32, :], T.zb[0:64, :]).then_inc(S["dw%d" % i], 32)
             a, b = sorted(tiles[i])
             for q, s in ((a, b), (b, a)):
-                Y.dma_start(T["wt%d" % i][32 * s:32 * s + 32, :], T.w[32 * q:32 * q + 32, :]).then_inc(S["dw%d" % i], 16)
+                Y.dma_start(wt[i][32 * s:32 * s + 32, :], T.w[32 * q:32 * q + 32, :]).then_inc(S["dw%d" % i], 16)
         elif x[0] == "z":
-            once(Y, "y", "fz", 1)
+            once(Y, "y", "fz", 2)
             if zrows(i) != slice(0, 128):
                 Y.dma_start(T["wt%d" % i][zrows(i), :], T.zb[:]).then_inc(S["dw%d" % i], 32)
                 continue
-            for s in sorted(set(range(N)) - tiles[i]):
-                Y.dma_start(T["wt%d" % i][32 * s:32 * s + 32, :], T.zb[0:64, :]).then_inc(S["dw%d" % i], 16)
+            a = 384 * fills.get(i, 0)
+            for s in sorted(set(range(N)) - tiles[i])[int(x[2])::2]:
+                Y.dma_start(T["wt%d" % i][32 * s:32 * s + 32, a:1536], T.zb[0:(1536 - a) // 24, :]).then_inc(S["dw%d" % i], 16)
+        elif x[0] == "a":
+            Y.wait_ge(S.loa, 1)
         elif x[0] == "l":
-            Y.wait_ge(S.lsent, ne + ne)
+            Y.wait_ge(S.lsent, 2 * ne)
+        elif x[0] == "c":
+            Y.wait_ge(S.csent, ne)
         else:
             Y.wait_ge(S["qe%d" % i], 1)
 
-    g.iota(T.pw[:], [[0, 12]], 0, 1).then_inc(S.iot, 1)
+    g.iota(T.pw[:], [[0, 24]], 0, 1).then_inc(S.iot, 1)
     adr = [topo.addr(d) for d in dsts]
-    g.wait_ge(S.loa, 1)
-    g.remote_dma(T.lin[:, 0:12], T.lout[:, 0:12], S.laa, S.lsent, adr[0][1], adr[0][0], mask)
-    g.wait_ge(S.lob, 1)
-    g.remote_dma_fused([RemoteDMATransfer(
-        dst_ids=[DstId(rid=adr[j][0], pnc=adr[j][1])], dma_engine_mask=halves[j - 1], remote_sem=S.lab,
-        srcs=[T.lout[:, 12 * j:12 * j + 12]], dsts=[T.lin[:, 12 * j:12 * j + 12]]) for j in (1, 2)], local_sem=S.lsent)
+    g.wait_ge(S.co, len(parts(2, False)))
+    g.remote_dma(T.cin[:], T.cout[:], S.lac, S.csent, adr[2][1], adr[2][0], mask)
+    for j, ready, landed in ((0, S.loa, S.laa), (1, S.lob, S.lab)):
+        g.wait_ge(ready, 1)
+        g.remote_dma(T.lin[:, 12 * j:12 * j + 12], T.lout[:, 12 * j:12 * j + 12], landed, S.lsent, adr[j][1], adr[j][0], mask)
     for j in range(3):
         rid, pid, _ = adr[j]
         g.wait_ge(S["qe%d" % j], 1)
@@ -139,23 +159,23 @@ def rank_program(g, core, T, topo):
     g.wait_ge(S.esent, 6 * ne)
 
     V.memset(T.xs[:], 0).then_inc(S.c0, 1)
-    V.memset(T.zb[:], 0.0).then_inc(S.fz, 1)
+    V.memset(T.cout[:], 0).then_inc(S.c0, 1)
+    V.memset(T.zb[:, 0:384], 0.0).then_inc(S.fz, 1)
     V.wait_ge(S.iot, 1)
     V.tensor_scalar(T.lw[:], T.pw[:], 16, None, AND).then_inc(S.c0, 1)
-    V.wait_ge(S.c0, 2)
+    V.memset(T.zb[:, 384:768], 0.0).then_inc(S.fz, 1)
+    V.wait_ge(S.c0, 3)
     V.tensor_copy(T.lf[:], T.lw[:]).then_inc(S.c1, 1)
-    for j in range(4):
-        f = 2.0 ** -SH[2 * qs[j]]
-        V.tensor_scalar(T.sc[:, j:j + 1], T.lw[:, 0:1], f / 16, f, MUL, ADD).then_inc(S.ka, 1)
+    for b, q in enumerate((q1, q2, r)):
+        f = 2.0 ** -SH[2 * q]
+        V.tensor_scalar(T.sc[:, b:b + 1], T.lw[:, 0:1], f / 16, f, MUL, ADD).then_inc(S.ka, 1)
 
     def shift(j, sem):
-        q = qs[j]
-        parts = [(0, 128, 0)] if q == 0 else [(0, 96, 0)] if q == 3 else [(0, 96, 0), (96, 128, M0[q])]
-        if j == 0 and q < 3:
-            parts = [[(32, 64, 0), (64, 128, 0)], [(0, 32, 0), (64, 96, 0), parts[-1]], [(0, 64, 0), parts[-1]]][q]
-        for a, b, m in parts:
-            V.tensor_scalar(T.xs[a:b, :, 12 * j:12 * j + C], T.cxy[a:b, :, m:m + C], T.sc[a:b, j:j + 1], 2.0 ** -8 - 0.5, MUL, ADD).then_inc(sem, 1)
-        return len(parts)
+        b, k = blk[j], min(blk[j], 2)
+        for p0, p1, m in parts(j, j == 0) if j != 2 else [(0, 128, 0)]:
+            V.tensor_scalar(T.xs[p0:p1, :, 12 * b:12 * b + C], (T.cxy if j != 2 else T.cin)[p0:p1, :, m:m + C],
+                            T.sc[p0:p1, k:k + 1], 2.0 ** -8 - 0.5, MUL, ADD).then_inc(sem, 1)
+        return len(parts(j, j == 0))
 
     def step(n, c, sem, cnt, done):
         V.wait_ge(sem, cnt)
@@ -171,18 +191,27 @@ def rank_program(g, core, T, topo):
     made = {"a": 0, "b": 0}
 
     def addresses(x, n):
-        if x == "s":
-            once(V, "v", "ka", 4)
-            once(V, "v", "lb" if n else "la", 64 if n else 192)
+        if x == "c":
+            once(V, "v", "lb", 64)
+            for p0, p1, m in parts(2, False):
+                V.tensor_copy(T.cout[p0:p1, :, 0:C], T.cxy[p0:p1, :, m:m + C]).then_inc(S.co, 1)
+        elif x == "s" and n == 2:
+            V.wait_ge(S.lac, ne)
+            shift(n, S.sr)
+        elif x == "s":
+            once(V, "v", "ka", 3)
+            once(V, "v", "la", 192)
             made["b" if n else "a"] += shift(n, S.sb if n else S.sa)
         elif x == "a":
             once(V, "v", "ma", 2)
             step(n, slice(0, 12), S.sa, made[x] + n, S.loa)
+        elif x == "b":
+            once(V, "v", "mb", 4)
+            step(n, slice(12, 36), S.sb, made[x] + n, S.lob)
         else:
-            once(V, "v", "mb", 6)
-            step(n, slice(12, 48), S.sb, made[x] + n, S.lob)
+            step(n, slice(36, 48), S.sr, 1 + n, S.loc)
 
-    lists = (("laa", ne), ("lab", ne), ("lab", ne), ("lob", 1))
+    lists = (("laa", ne), ("lab", ne), ("loc", 1), ("lob", 1))
     cnt = {e: [plans.count("g%d" % j) for j in range(4)] for e, plans in (("v", VPLAN), ("a", APLAN))}
 
     def call(Q, name, x):
@@ -194,7 +223,7 @@ def rank_program(g, core, T, topo):
             if name == "v":
                 V.memset(out, 0.0).then_inc(S["fw%d" % i], n)
             else:
-                once(A, name, "fz", 1)
+                once(A, name, "fz", 2)
                 copy(out, T.zb[zrows(i), 0:384 * n]).then_inc(S["fw%d" % i], n)
         elif x[0] == "d":
             once(Q, name, "tbs", 64)
@@ -202,7 +231,7 @@ def rank_program(g, core, T, topo):
         elif x[0] == "g":
             once(Q, name, "pl%d" % t, 1)
             once(Q, name, *lists[i])
-            off = (T.lin if i < 3 else T.lout)[:, 12 * i:12 * i + C]
+            off = (T.lin if i < 2 else T.lout)[:, 12 * blk[i]:12 * blk[i] + C]
             copy(T["eb%d" % i][:, t:4 * NC:4], T.tbp[:, K * t:K * t + K].indirect(off)).then_inc(S[("gv%d" if name == "v" else "gs%d") % i], 1)
         elif x[0] == "q":
             for e, sem in (("a", "gs%d"), ("v", "gv%d")):
@@ -211,9 +240,9 @@ def rank_program(g, core, T, topo):
             V.quantize_mx(T["eq%d" % i][:], T["es%d" % i][:], T["eb%d" % i][:]).then_inc(S["qe%d" % i], 1)
         elif x[0] == "w":
             if i in fills:
-                V.wait_ge(S["fw%d" % i], 4)
-            V.wait_ge(S["dw%d" % i], 32 if i in fills else 64)
-            V.quantize_mx(T["wq%d" % i][:], T["ws%d" % i][:], T["wt%d" % i][:]).then_inc(S["qw%d" % i], 1)
+                V.wait_ge(S["fw%d" % i], fills[i])
+            V.wait_ge(S["dw%d" % i], 32 if fills.get(i) == 4 else 64)
+            V.quantize_mx(T["wq%d" % i][:], T["ws%d" % i][:], wt[i][:]).then_inc(S["qw%d" % i], 1)
         elif x[0] == "p":
             A.wait_ge(S.pa, 1)
             copy(T.part[:, 0:NC - lo[t8]], T.acc[:, 3584:3584 + NC - lo[t8]]).then_inc(S.pb, 1)
@@ -224,10 +253,10 @@ def rank_program(g, core, T, topo):
         call(V, "v", x)
 
     A.wait_ge(S.c1, 1)
-    for j in range(4):
-        a, b = 2 * qs[j], 2 * qs[j] + 1
+    for j, (q, n) in enumerate(((q1, 12), (q2, 12), (r, 24))):
         for c, M in ((0, MA), (1, MB)):
-            A.activation(T.ab[:, c, 12 * j:12 * j + 12], T.lf[:], IDENT, bias=float(M[a]), scale=(M[b] - M[a]) / 16.0).then_inc(S.mb if j else S.ma, 1)
+            A.activation(T.ab[:, c, 12 * j:12 * j + n], T.lf[:, 0:n], IDENT, bias=float(M[2 * q]),
+                         scale=(M[2 * q + 1] - M[2 * q]) / 16.0).then_inc(S.mb if j else S.ma, 1)
     for x in APLAN.split():
         call(A, "a", x)
 

from concourse.bass import DstId, RemoteDMATransfer
from concourse.mybir import dt, AluOpType, ActivationFunctionType

N = 4
O = 3
SH = (7, 6, 5, 4, 3, 2, 1, 0)
MA = (1531, 797, 1877, 1129, 619, 1993, 1367, 911)
MB = (1013, 1741, 587, 1459, 1907, 733, 1229, 1667)
K = 512
M0 = (0, 11, 21)
C = 11
NC = 16 * C
F8 = "float8_e4m3fn_x4"

SCRATCH = {
    "cxy": ("sbuf", [128, 2, 32], "int32"),
    "cout": ("sbuf", [128, 2, 12], "uint16"), "cin": ("sbuf", [128, 2, 12], "uint16"),
    "pw": ("sbuf", [128, 24], "int32"), "lw": ("sbuf", [128, 24], "int32"), "lf": ("sbuf", [128, 24], "float32"),
    "ab": ("sbuf", [128, 2, 48], "float32"), "sc": ("sbuf", [128, 4], "float32"),
    "xs": ("sbuf", [128, 2, 48], "int32"), "xm": ("sbuf", [128, 2, 48], "float32"),
    "xa": ("sbuf", [128, 48], "int32"), "adr": ("sbuf", [128, 48], "int32"),
    "lout": ("sbuf", [128, 48], "uint16"), "lin": ("sbuf", [128, 48], "uint16"),
    "tbl": ("sbuf", [128, 4 * K], "bfloat16"), "tbp": ("sbuf", [128, 4 * K], "bfloat16"), "zb": ("sbuf", [128, 768], "bfloat16"),
    "yb": ("sbuf", [128, 1536], "float32"), "part": ("sbuf", [128, NC], "float32"),
    "acc": ("psum", [128, 4096], "float32"),
}
for _i in range(6):
    SCRATCH["wt%d" % _i] = ("sbuf", [128, 1536], "bfloat16")
    SCRATCH["wq%d" % _i] = ("sbuf", [128, 384], F8)
    SCRATCH["ws%d" % _i] = ("sbuf", [128, 384], "uint8")
for _j in range(4):
    SCRATCH["eb%d" % _j] = ("sbuf", [128, 4 * NC], "bfloat16")
    SCRATCH["eq%d" % _j] = ("sbuf", [128, NC], F8)
    SCRATCH["es%d" % _j] = ("sbuf", [128, NC], "uint8")
    if _j < 3:
        SCRATCH["rq%d" % _j] = ("sbuf", [128, NC], F8)
        SCRATCH["rs%d" % _j] = ("sbuf", [128, NC], "uint8")

SEMAPHORES = (["la", "lb", "fz", "tbs", "iot", "c0", "c1", "ka", "ma", "mb", "sa", "sb", "loa", "lob",
               "laa", "lab", "lac", "loc", "co", "sr", "csent", "lsent", "esent", "sf", "vf", "ys", "pa", "pb"]
              + ["%s%d" % (n, k) for n in ("gv", "gs", "qe", "pl", "arr") for k in range(4)]
              + ["%s%d" % (n, i) for n in ("fw", "dw", "qw") for i in range(6)]
              + ["pp%d" % b for b in range(9)])

YPLAN = "w0 z0 z40 w1 c0 w3 z41 w4 w5 w20 l0"
VPLAN = "f101 s0 c0 s1 a0 s3 a1 b0 a2 f12 b1 a3 d1 b2 f13 b3 d2 d3 w0 g30 s2 g00 r0 g01 r1 q3 q0 r2 g10 r3 w1 q1 g20 g21 q2 w3 w2 w4 w5"
APLAN = "f301 f323 d0 g31 g32 g33 g02 g03 g11 g12 g13 g22 g23 f501 p00 f523"
PPLAN = "30 31 00 03 32 04 11 13 15"
STORES = "0 12 345 678"

ADD, MUL, AND = AluOpType.add, AluOpType.mult, AluOpType.bitwise_and
COPY, IDENT = ActivationFunctionType.Copy, ActivationFunctionType.Identity


def rank_program(g, core, T, topo):
    r = T.rank_of(core)
    if r is None:
        return
    S = T.sem
    V, A, P, Y = g.vector, g.scalar, g.tensor, g.sync
    ks = sorted((1, 2, 3), key=lambda k: topo.same_plane(topo.chip(core), topo.chip(T.cores[r ^ k])))
    qs = [r ^ k for k in ks] + [r]
    q1, q2, q3 = qs[:3]
    tiles = [{r, q1}, {r, q2}, {r, q3}, {q1, q2}, {q1, q3}, {q2, q3}]
    dsts = [T.cores[q] for q in qs[:3]]
    engs = [e for e in topo.engines(core, dsts[0]) if all(e in topo.engines(core, d) for d in dsts)]
    ne = len(engs)
    mask = sum(1 << e for e in engs)
    halves = [sum(1 << e for e in engs[h::2]) for h in range(2)]

    lo = (0, 0, 16 * (M0[1] + C - M0[2]))

    def third(j, i):
        s = min(tiles[i] - {qs[j]})
        return s if s < 3 else qs[j]

    def tile_of(j, th):
        return [i for i in range(6) if qs[j] in tiles[i] and third(j, i) == th][0]

    plan = [(int(x[0]), int(x[1])) for x in PPLAN.split()]
    own = [third(j, i) for j, i in plan if j == 3]
    t8 = own[0] if own[0] != 1 else own[1]
    seq = [(o, th) for o in range(O - 1) for th in range(3)] + [(O - 1, th) for th in (own[0] + own[1] - t8, own[2], t8)]
    met = []

    def once(queue, name, sem, n):
        if (name, sem) not in met:
            met.append((name, sem))
            queue.wait_ge(S[sem], n)

    blk = (0, 1, 3, 2)

    def parts(j, bare):
        q = qs[j]
        last = (96, 128, M0[q % 3])
        if bare:
            return [[(32, 64, 0), (64, 128, 0)], [(0, 32, 0), (64, 96, 0), last], [(0, 64, 0), last], [(0, 96, 0)]][q]
        return [(0, 128, 0)] if q == 0 else [(0, 96, 0)] if q == 3 else [(0, 96, 0), last]

    def zrows(i):
        if tiles[i] in ({0, 1}, {2, 3}):
            return slice(64, 128) if 0 in tiles[i] else slice(0, 64)
        return slice(0, 128)

    for s in sorted(range(4), key=lambda s: s == q1):
        for l in range(2):
            p = 32 * s + 16 * l
            m, n = (M0[s], C) if s < 3 else (0, 32)
            Y.dma_start(T.cxy[p:p + 16, 0, 0:n], T.px[:, m:m + n]).then_inc(S.lb if s == q1 else S.la, 16)
            A.dma_start(T.cxy[p:p + 16, 1, 0:n], T.py[:, m:m + n]).then_inc(S.lb if s == q1 else S.la, 16)
    for s in range(4):
        q = r if s != r else (r + 1) % N
        (Y, A)[s % 2].dma_start(T.tbl[32 * s:32 * s + 32, :], T.tb[32 * q:32 * q + 32, :]).then_inc(S.tbs, 16)

    fills = {i: sum(len(x) - 2 for x in (VPLAN + " " + APLAN).split() if x[:2] == "f%d" % i) for i in range(6) if "f%d0" % i in VPLAN + APLAN}
    after = {int(x[1]): int(x[2]) for x in YPLAN.split() if x[0] == "w" and len(x) == 3}
    wt = [T["wt%d" % after.get(i, i)] for i in range(6)]
    for x in YPLAN.split():
        i = int(x[1])
        if x[0] == "w":
            if i in fills and zrows(i) == slice(0, 128):
                Y.wait_ge(S["fw%d" % i], fills[i])
            if i in after:
                Y.wait_ge(S["qw%d" % after[i]], 1)
                s = min(tiles[after[i]] - tiles[i])
                Y.dma_start(wt[i][32 * s:32 * s + 32, :], T.zb[0:64, :]).then_inc(S["dw%d" % i], 32)
            a, b = sorted(tiles[i])
            for q, s in ((a, b), (b, a)):
                Y.dma_start(wt[i][32 * s:32 * s + 32, :], T.w[32 * q:32 * q + 32, :]).then_inc(S["dw%d" % i], 16)
        elif x[0] == "z":
            once(Y, "y", "fz", 2)
            if zrows(i) != slice(0, 128):
                Y.dma_start(T["wt%d" % i][zrows(i), :], T.zb[:]).then_inc(S["dw%d" % i], 32)
                continue
            a = 384 * fills.get(i, 0)
            for s in sorted(set(range(N)) - tiles[i])[int(x[2])::2]:
                Y.dma_start(T["wt%d" % i][32 * s:32 * s + 32, a:1536], T.zb[0:(1536 - a) // 24, :]).then_inc(S["dw%d" % i], 16)
        elif x[0] == "a":
            Y.wait_ge(S.loa, 1)
        elif x[0] == "l":
            Y.wait_ge(S.lsent, 2 * ne)
        elif x[0] == "c":
            Y.wait_ge(S.csent, ne)
        else:
            Y.wait_ge(S["qe%d" % i], 1)

    g.iota(T.pw[:], [[0, 24]], 0, 1).then_inc(S.iot, 1)
    adr = [topo.addr(d) for d in dsts]
    g.wait_ge(S.co, len(parts(2, False)))
    g.remote_dma(T.cin[:], T.cout[:], S.lac, S.csent, adr[2][1], adr[2][0], mask)
    for j, ready, landed in ((0, S.loa, S.laa), (1, S.lob, S.lab)):
        g.wait_ge(ready, 1)
        g.remote_dma(T.lin[:, 12 * j:12 * j + 12], T.lout[:, 12 * j:12 * j + 12], landed, S.lsent, adr[j][1], adr[j][0], mask)
    for j in range(3):
        rid, pid, _ = adr[j]
        g.wait_ge(S["qe%d" % j], 1)
        g.remote_dma(T["rq%d" % j][:].bitcast(dt.uint8), T["eq%d" % j][:].bitcast(dt.uint8), S["arr%d" % j], S.esent, pid, rid, mask)
        g.remote_dma(T["rs%d" % j][:], T["es%d" % j][:], S["arr%d" % j], S.esent, pid, rid, mask)
    g.wait_ge(S.esent, 6 * ne)

    V.memset(T.xs[:], 0).then_inc(S.c0, 1)
    V.memset(T.cout[:], 0).then_inc(S.c0, 1)
    V.memset(T.zb[:, 0:384], 0.0).then_inc(S.fz, 1)
    V.wait_ge(S.iot, 1)
    V.tensor_scalar(T.lw[:], T.pw[:], 16, None, AND).then_inc(S.c0, 1)
    V.memset(T.zb[:, 384:768], 0.0).then_inc(S.fz, 1)
    V.wait_ge(S.c0, 3)
    V.tensor_copy(T.lf[:], T.lw[:]).then_inc(S.c1, 1)
    for b, q in enumerate((q1, q2, r)):
        f = 2.0 ** -SH[2 * q]
        V.tensor_scalar(T.sc[:, b:b + 1], T.lw[:, 0:1], f / 16, f, MUL, ADD).then_inc(S.ka, 1)

    def shift(j, sem):
        b, k = blk[j], min(blk[j], 2)
        for p0, p1, m in parts(j, j == 0) if j != 2 else [(0, 128, 0)]:
            V.tensor_scalar(T.xs[p0:p1, :, 12 * b:12 * b + C], (T.cxy if j != 2 else T.cin)[p0:p1, :, m:m + C],
                            T.sc[p0:p1, k:k + 1], 2.0 ** -8 - 0.5, MUL, ADD).then_inc(sem, 1)
        return len(parts(j, j == 0))

    def step(n, c, sem, cnt, done):
        V.wait_ge(sem, cnt)
        if n == 0:
            V.tensor_tensor(T.xm[:, :, c], T.xs[:, :, c], T.ab[:, :, c], MUL).then_inc(sem, 1)
        elif n == 1:
            V.tensor_tensor(T.xa[:, c], T.xm[:, 0, c], T.xm[:, 1, c], ADD).then_inc(sem, 1)
        elif n == 2:
            V.tensor_scalar(T.adr[:, c], T.xa[:, c], K - 1, None, AND).then_inc(sem, 1)
        else:
            V.tensor_copy(T.lout[:, c], T.adr[:, c]).then_inc(done, 1)

    made = {"a": 0, "b": 0}

    def addresses(x, n):
        if x == "c":
            once(V, "v", "lb", 64)
            for p0, p1, m in parts(2, False):
                V.tensor_copy(T.cout[p0:p1, :, 0:C], T.cxy[p0:p1, :, m:m + C]).then_inc(S.co, 1)
        elif x == "s" and n == 2:
            V.wait_ge(S.lac, ne)
            shift(n, S.sr)
        elif x == "s":
            once(V, "v", "ka", 3)
            once(V, "v", "la", 192)
            made["b" if n else "a"] += shift(n, S.sb if n else S.sa)
        elif x == "a":
            once(V, "v", "ma", 2)
            step(n, slice(0, 12), S.sa, made[x] + n, S.loa)
        elif x == "b":
            once(V, "v", "mb", 4)
            step(n, slice(12, 36), S.sb, made[x] + n, S.lob)
        else:
            step(n, slice(36, 48), S.sr, 1 + n, S.loc)

    lists = (("laa", ne), ("lab", ne), ("loc", 1), ("lob", 1))
    cnt = {e: [plans.count("g%d" % j) for j in range(4)] for e, plans in (("v", VPLAN), ("a", APLAN))}

    def call(Q, name, x):
        i, t = int(x[1]), int(x[-1])
        copy = V.tensor_copy if name == "v" else lambda out, in_: A.activation(out, in_, COPY)
        if x[0] == "f":
            a, n = int(x[2]), len(x) - 2
            out = T["wt%d" % i][zrows(i), 384 * a:384 * (a + n)]
            if name == "v":
                V.memset(out, 0.0).then_inc(S["fw%d" % i], n)
            else:
                once(A, name, "fz", 2)
                copy(out, T.zb[zrows(i), 0:384 * n]).then_inc(S["fw%d" % i], n)
        elif x[0] == "d":
            once(Q, name, "tbs", 64)
            copy(T.tbp[:, K * t:K * t + K], T.tbl[:, t:4 * K:4]).then_inc(S["pl%d" % t], 1)
        elif x[0] == "g":
            once(Q, name, "pl%d" % t, 1)
            once(Q, name, *lists[i])
            off = (T.lin if i < 2 else T.lout)[:, 12 * blk[i]:12 * blk[i] + C]
            copy(T["eb%d" % i][:, t:4 * NC:4], T.tbp[:, K * t:K * t + K].indirect(off)).then_inc(S[("gv%d" if name == "v" else "gs%d") % i], 1)
        elif x[0] == "q":
            for e, sem in (("a", "gs%d"), ("v", "gv%d")):
                if cnt[e][i]:
                    V.wait_ge(S[sem % i], cnt[e][i])
            V.quantize_mx(T["eq%d" % i][:], T["es%d" % i][:], T["eb%d" % i][:]).then_inc(S["qe%d" % i], 1)
        elif x[0] == "w":
            if i in fills:
                V.wait_ge(S["fw%d" % i], fills[i])
            V.wait_ge(S["dw%d" % i], 32 if fills.get(i) == 4 else 64)
            V.quantize_mx(T["wq%d" % i][:], T["ws%d" % i][:], wt[i][:]).then_inc(S["qw%d" % i], 1)
        elif x[0] == "p":
            A.wait_ge(S.pa, 1)
            copy(T.part[:, 0:NC - lo[t8]], T.acc[:, 3584:3584 + NC - lo[t8]]).then_inc(S.pb, 1)
        else:
            addresses(x[0], i)

    for x in VPLAN.split():
        call(V, "v", x)

    A.wait_ge(S.c1, 1)
    for j, (q, n) in enumerate(((q1, 12), (q2, 12), (r, 24))):
        for c, M in ((0, MA), (1, MB)):
            A.activation(T.ab[:, c, 12 * j:12 * j + n], T.lf[:, 0:n], IDENT, bias=float(M[2 * q]),
                         scale=(M[2 * q + 1] - M[2 * q]) / 16.0).then_inc(S.mb if j else S.ma, 1)
    for x in APLAN.split():
        call(A, "a", x)

    begun = []

    def mm(j, i, o, last):
        e, z = ("rq%d", "rs%d") if j < 3 else ("eq%d", "es%d")
        once(P, "p", "qw%d" % i, 1)
        once(P, "p", "arr%d" % j if j < 3 else "qe3", 2 * ne if j < 3 else 1)
        th = third(j, i)
        n = seq.index((o, th))
        first = n not in begun or (n, j) == (8, 0)
        if first and n == 7:
            P.wait_ge(S.pb, 1)
        begun.append(n)
        c = slice(128 * o, 128 * o + 128)
        b = 512 * (n if n < 8 else 7 if j == 3 else 0)
        return P.matmul_mx(T.acc[:, b:b + NC - lo[th]], T["wq%d" % i][:, c], T["ws%d" % i][:, c],
                           T[e % j][:, lo[th]:NC], T[z % j][:, lo[th]:NC], first, last)

    for j, i in plan:
        for o in range(O):
            x = (o, third(j, i))
            if (j, x) == (3, seq[8]):
                mm(j, i, o, True).then_inc(S.pa, 1)
            elif x != seq[8]:
                mm(j, i, o, False)
    for n, (o, th) in enumerate(seq):
        if n == 8:
            P.wait_ge(S.vf, 1)
            for j in (0, 1):
                mm(j, tile_of(j, th), o, False)
        mm(2, tile_of(2, th), o, True).then_inc(S["pp%d" % n], 1)

    num = {"sf": 0, "vf": 0}
    done, cols = [], []
    for n, (o, th) in enumerate(seq):
        cols.append((512 * o + 16 * M0[th] + lo[th], 512 * o + 16 * M0[th] + NC))
        y = T.yb[:, cols[n][0]:cols[n][1]]
        a = T.acc[:, 512 * (n % 8):512 * (n % 8) + NC - lo[th]]
        if n % 2:
            A.wait_ge(S["pp%d" % n], 1)
            A.activation(y, a, COPY).then_inc(S.sf, 1)
        else:
            V.wait_ge(S["pp%d" % n], 1)
            if n < 8:
                V.tensor_copy(y, a).then_inc(S.vf, 1)
            else:
                V.wait_ge(S.pb, 1)
                V.tensor_tensor(y, a, T.part[:, 0:NC - lo[th]], ADD).then_inc(S.vf, 1)
        num["sf" if n % 2 else "vf"] += 1
        done.append(dict(num))
    stores, got = 0, {"sf": 0, "vf": 0}
    for x in STORES.split():
        runs = sorted(cols[int(n)] for n in x)
        for sem, n in done[int(x[-1])].items():
            if n > got[sem]:
                Y.wait_ge(S[sem], n)
                got[sem] = n
        while runs:
            a, b = runs.pop(0)
            while runs and runs[0][0] == b:
                b = runs.pop(0)[1]
            Y.dma_start(T.y[:, a:b], T.yb[:, a:b]).then_inc(S.ys, 16)
            stores += 1
    Y.wait_ge(S.ys, 16 * stores)
